import numpy as np
import ml_dtypes


def mxq(x, axis, fmt="e4m3"):
    dtype, down = {"e4m3": (ml_dtypes.float8_e4m3fn, 7), "e5m2": (ml_dtypes.float8_e5m2, 14)}[fmt]
    v = np.moveaxis(np.asarray(x, np.float32).astype(ml_dtypes.bfloat16).astype(np.float64), axis, -1)
    blocks = v.reshape(v.shape[:-1] + (-1, 32))
    amax = np.abs(blocks).max(-1, keepdims=True)
    byte = np.maximum(np.where(amax > 0, np.frexp(amax)[1] - 1 + 127, 0) - down, 1)
    scale = np.exp2(byte - 127.0)
    codes = (blocks / scale).astype(np.float32).astype(dtype).astype(np.float64)
    return np.moveaxis((codes * scale).reshape(v.shape), -1, axis)


WIDE = False


def mx_kscale(k):
    if not WIDE:
        return np.ones(k)
    levels = np.array([10, -10, 5, -5, 0])
    if k % 512:
        return np.exp2(np.random.permutation(np.resize(levels, k // 32))).repeat(32)
    a = np.empty((k // 512, 16))
    for p in range(k // 512):
        a[p, :8] = np.random.permutation(np.resize(levels, 8))
        for g in range(8):
            far = levels[np.abs(levels - a[p, g]) >= 10]
            a[p, g + 8] = far[np.random.randint(len(far))]
    return np.exp2(a.ravel()).repeat(32)


BF16 = ml_dtypes.bfloat16


def bf(x):
    return np.asarray(x, np.float32).astype(BF16)


def f64(x):
    return np.asarray(x).astype(np.float64)


E2M1 = np.array([0.0, 0.5, 1.0, 1.5, 2.0, 3.0, 4.0, 6.0, -0.0, -0.5, -1.0, -1.5, -2.0, -3.0, -4.0, -6.0])


def pack_weight(w, fmt):
    k, n = w.shape
    w = f64(bf(w)).reshape(k // 32, 32, n)
    amax = np.abs(w).max(1)
    if fmt == "e4m3":
        byte = np.frexp(amax)[1] - 1 + 127 - 7
    else:
        mant, ex = np.frexp(amax / 6.0)
        byte = np.where(mant > 0.5, ex, ex - 1) + 127
    byte = np.clip(np.where(amax > 0, byte, 1), 1, 254)
    scaled = (w * np.exp2(127.0 - byte)[:, None, :]).reshape(k, n).astype(np.float32)
    by_word = np.ascontiguousarray(scaled.reshape(k // 512, 128, 4, n).transpose(0, 1, 3, 2))
    if fmt == "e4m3":
        words = by_word.astype(ml_dtypes.float8_e4m3fn).view(np.uint8)
    else:
        c = by_word.astype(ml_dtypes.float4_e2m1fn).view(np.uint8) & 0xF
        words = c[..., 0::2] | (c[..., 1::2] << 4)
    return np.ascontiguousarray(words), np.ascontiguousarray(byte.astype(np.uint8).reshape(k // 512, 16, n))


def unpack_weight(words, scales, fmt):
    g, p, n, _ = words.shape
    if fmt == "e4m3":
        vals = np.ascontiguousarray(words).view(ml_dtypes.float8_e4m3fn).astype(np.float64)
    else:
        nib = np.empty((g, p, n, 4), np.uint8)
        nib[..., 0::2] = words & 0xF
        nib[..., 1::2] = words >> 4
        vals = E2M1[nib]
    vals = vals * np.repeat(np.exp2(scales.astype(np.float64) - 127.0), 8, axis=1)[..., None]
    return vals.transpose(0, 1, 3, 2).reshape(g * 512, n)
def pack4(w):
    words, scales = pack_weight(w, "e2m1")
    return words.reshape(words.shape[0], 128, -1), scales


def unpack4(words, scales):
    return unpack_weight(words.reshape(words.shape[0], 128, -1, 2), scales, "e2m1")


E, D, V = 1024, 2048, 512


def draw0():
    s = mx_kscale(E)
    t = mx_kscale(D)
    keys = np.random.standard_normal((E, D)) * s[:, None] * t
    resid = np.random.standard_normal((E, V)) / np.sqrt(E) / s[:, None]
    c = np.random.standard_normal((D, D)) / np.sqrt(D) / t[:, None]
    cinv_words, cinv_scales = pack4(c)
    return {"keys": bf(keys),
            "resid": bf(resid),
            "inv_std": bf(np.exp(0.3 * np.random.standard_normal(D))),
            "cinv_words": cinv_words,
            "cinv_scales": cinv_scales,
            "w_old": bf(0.5 * np.random.standard_normal((D, V)))}


def core(keys, resid, inv_std, cinv_words, cinv_scales, w_old):
    d = f64(inv_std)[:, None]
    kq = mxq(f64(keys), 0, "e4m3")
    rq = mxq(f64(resid), 0, "e4m3")
    h = (kq.T @ rq) * d
    c = unpack4(cinv_words, cinv_scales)
    delta = c.T @ mxq(h, 0, "e4m3")
    return f64(w_old) + delta * d


def e4m3fn_bytes(y):
    return np.clip(np.asarray(y, np.float64), -448.0, 448.0).astype(np.float32).astype(ml_dtypes.float8_e4m3fn).view(np.uint8)


def e4m3fn_values(b):
    return np.asarray(b, np.uint8).view(ml_dtypes.float8_e4m3fn).astype(np.float64)


def setup_inputs():
    d = draw0()
    x0 = np.asarray(d['resid']).astype(np.float64)
    s = (np.max(np.abs(x0), axis=(1,), keepdims=True) / 448.0).astype(np.float32)
    out = {}
    for k, v in d.items():
        if k == 'resid':
            out['resid_bytes'] = e4m3fn_bytes(x0 / s.astype(np.float64))
            out['resid_scale'] = s
        else:
            out[k] = v
    return out


def reference(keys, resid_bytes, resid_scale, inv_std, cinv_words, cinv_scales, w_old):
    return core(keys, e4m3fn_values(resid_bytes) * resid_scale.astype(np.float64), inv_std, cinv_words, cinv_scales, w_old)

@@ -1,0 +1,435 @@
+from contextlib import ExitStack
+
+import concourse.mybir as mybir
+from concourse.masks import make_identity
+
+F32 = mybir.dt.float32
+BF16 = mybir.dt.bfloat16
+U32 = mybir.dt.uint32
+U8 = mybir.dt.uint8
+I32 = mybir.dt.int32
+E4M3 = mybir.dt.float8_e4m3fn
+E4M3X4 = mybir.dt.float8_e4m3fn_x4
+E2M1X4 = mybir.dt.float4_e2m1fn_x4
+MULT = mybir.AluOpType.mult
+ADD = mybir.AluOpType.add
+COPY = mybir.ActivationFunctionType.Copy
+
+P = 128
+E, D, V = 1024, 2048, 512
+NA = E // 512
+NG = D // 512
+NJ = D // P
+FLOPS = 2 * E * D * V + 2 * D * D * V
+
+
+def tile_memit_weight_edit_s13_kernel(
+    tc, keys, resid_bytes, resid_scale, inv_std, cinv_words, cinv_scales, w_old, out
+):
+    nc = tc.nc
+    with ExitStack() as ctx:
+        keep = ctx.enter_context(tc.tile_pool(name="keep", bufs=1))
+        psum = ctx.enter_context(tc.psum_pool(name="psum", bufs=1))
+
+        def sb(shape, dtype, name):
+            return keep.tile(shape, dtype, name=name, align_bytes=64)
+
+        def bank(i, shape, dtype, name):
+            return psum.tile(shape, dtype, name=name, tag="bank%d" % i)
+
+        raw = [[sb([P, 4, 512], BF16, "raw%d%d" % (g, a)) for a in range(NA)] for g in range(NG)]
+        grp = [[sb([P, 2048], BF16, "grp%d%d" % (g, a)) for a in range(NA)] for g in range(NG)]
+        kc = [[sb([P, 512], U32, "kc%d%d" % (g, a)) for a in range(NA)] for g in range(NG)]
+        ks = [[sb([P, 512], U8, "ks%d%d" % (g, a)) for a in range(NA)] for g in range(NG)]
+        r8 = [sb([P, 4, 512], U8, "r8%d" % a) for a in range(NA)]
+        rw = [sb([P, 4, 512], BF16, "rw%d" % a) for a in range(NA)]
+        rg = [sb([P, 2048], BF16, "rg%d" % a) for a in range(NA)]
+        rc = [sb([P, 512], U32, "rc%d" % a) for a in range(NA)]
+        rs = [sb([P, 512], U8, "rs%d" % a) for a in range(NA)]
+        hg = [sb([P, 2048], BF16, "hg%d" % g) for g in range(NG)]
+        hc = [sb([P, 512], U32, "hc%d" % g) for g in range(NG)]
+        hs = [sb([P, 512], U8, "hs%d" % g) for g in range(NG)]
+        cw = [sb([P, 4096], U8, "cw%d" % g) for g in range(NG)]
+        cs = sb([P, NG * 2048], U8, "cs")
+        w = [sb([P, 4, 512], BF16, "w%d" % i) for i in range(4)]
+        ident = sb([P, P], BF16, "ident")
+        rscale = sb([P, NA, 4], F32, "rscale")
+        d1raw = sb([P, NG, 4], BF16, "d1raw")
+        d1 = sb([P, NG, 4], F32, "d1")
+        drow = sb([P, P], BF16, "drow")
+        drow_z = sb([P, P], BF16, "drow_z")
+        d2 = sb([P, NJ], F32, "d2")
+        tiny = sb([P, 1], F32, "tiny")
+        tiny2 = sb([P, 1], F32, "tiny2")
+
+        ctx.enter_context(tc.manual_schedule())
+
+        nc.gpsimd.memset(tiny[:], 0.0)
+        make_identity(nc, ident[:])
+        nc.gpsimd.memset(drow[:], 0.0)
+        nc.gpsimd.memset(drow_z[:], 0.0)
+        nc.gpsimd.memset(cs[:].bitcast(I32), 0)
+        nc.scalar.dma_start(out=rscale[:], in_=resid_scale.rearrange("(a p t) o -> p a (t o)", a=NA, t=4))
+        nc.scalar.activation(out=tiny2[:], in_=tiny[:], func=COPY)
+        nc.scalar.dma_start(out=d1raw[:], in_=inv_std.rearrange("(g p t) -> p g t", g=NG, t=4))
+        nc.scalar.dma_start(out=drow[0:NJ, :], in_=inv_std.rearrange("(j p) -> j p", p=P))
+
+        r8_in = resid_bytes.rearrange("(a p t) n -> a p t n", a=NA, t=4)
+        keys_in = keys.rearrange("(a p t) i -> a p t i", a=NA, t=4)
+        w_in = w_old.rearrange("(b q p) v -> b p q v", q=4, p=P)
+        cs_in = cinv_scales.bitcast(I32)
+        cs_w = cs[:].bitcast(I32)
+
+        def load_keys(g):
+            for a in range(NA):
+                nc.sync.dma_start(out=raw[g][a][:], in_=keys_in[a][:, :, 512 * g : 512 * (g + 1)])
+
+        for a in range(NA):
+            nc.sync.dma_start(out=r8[a][:], in_=r8_in[a])
+        load_keys(0)
+        load_keys(1)
+        load_keys(2)
+        load_keys(3)
+        for q in range(4):
+            nc.sync.dma_start(
+                out=cs_w[32 * q : 32 * q + 4, :].rearrange("p (g n) -> p g n", g=NG),
+                in_=cs_in[:, 4 * q : 4 * q + 4, :].rearrange("g q n -> q g n"),
+            )
+        nc.sync.dma_start(out=cw[0][:], in_=cinv_words[0])
+        nc.sync.dma_start(out=cw[1][:], in_=cinv_words[1])
+        nc.sync.dma_start(out=cw[2][:], in_=cinv_words[2])
+        nc.sync.dma_start(out=cw[3][:], in_=cinv_words[3])
+        for i in range(4):
+            nc.sync.dma_start(out=w[i][:], in_=w_in[i])
+
+        def widen(eng, a, t):
+            src = r8[a][:, t, :].bitcast(E4M3)
+            if eng == "v":
+                nc.vector.tensor_scalar(out=rw[a][:, t, :], in0=src, scalar1=rscale[:, a, t : t + 1], scalar2=None, op0=MULT)
+            else:
+                nc.scalar.activation(out=rw[a][:, t, :], in_=src, func=COPY, scale=rscale[:, a, t : t + 1])
+
+        def copy(eng, dst, src):
+            if eng == "v":
+                nc.vector.tensor_copy(out=dst, in_=src)
+            else:
+                nc.scalar.copy(out=dst, in_=src)
+
+        def r_turn(a, h, b):
+            ps = bank(b, [P, 1024], BF16, "pr%d%d" % (a, h))
+            for u in range(2):
+                n0 = 256 * h + 128 * u
+                nc.tensor.matmul(
+                    out=ps[:, 512 * u : 512 * (u + 1)].rearrange("p (n t) -> p n t", t=4),
+                    lhsT=ident[:],
+                    rhs=rw[a][:, :, n0 : n0 + 128].rearrange("p t n -> p n t"),
+                    start=True,
+                    stop=True,
+                )
+            return ps
+
+        def k_view(g, a, t0, t1):
+            return raw[g][a][:].rearrange("p j (m t) -> p t m j", t=4)[:, t0:t1]
+
+        def k_turn(g, a, t0, b):
+            ps = bank(b, [P, 1024], BF16, "pk%d%d%d" % (g, a, t0))
+            for u in range(2):
+                nc.tensor.matmul(
+                    out=ps[:, 512 * u : 512 * (u + 1)].rearrange("p (m j) -> p m j", j=4),
+                    lhsT=ident[:],
+                    rhs=raw[g][a][:].rearrange("p j (m t) -> p t m j", t=4)[:, t0 + u],
+                    start=True,
+                    stop=True,
+                )
+            return ps
+
+        def k_direct(eng, g, a, t0, t1):
+            copy(
+                eng,
+                grp[g][a][:, 512 * t0 : 512 * t1].rearrange("p (t m j) -> p t m j", m=128, j=4),
+                k_view(g, a, t0, t1),
+            )
+
+        def k_out(eng, g, a, t0, ps):
+            copy(eng, grp[g][a][:, 512 * t0 : 512 * t0 + 1024], ps[:])
+
+        def quant(codes, scales, src, c=slice(0, 512)):
+            nc.vector.quantize_mx(
+                out=codes[:, c].bitcast(E4M3X4), scales=scales[:, c], in_=src[:, 4 * c.start : 4 * c.stop]
+            )
+
+        def quant_k(g, a):
+            quant(kc[g][a], ks[g][a], grp[g][a])
+
+        def quant_r(a, h):
+            quant(rc[a], rs[a], rg[a], slice(256 * h, 256 * (h + 1)))
+
+        def quant_h(g):
+            quant(hc[g], hs[g], hg[g])
+
+        def stage1(g, q, b):
+            st = bank(b, [P, 4, P], F32, "st%d%d" % (g, q))
+            v = slice(P * q, P * (q + 1))
+            for t in range(4):
+                c = slice(P * t, P * (t + 1))
+                for a in range(NA):
+                    nc.tensor.matmul_mx(
+                        out=st[:, t, :],
+                        lhsT=kc[g][a][:, c].bitcast(E4M3X4),
+                        lhsT_scale=ks[g][a][:, c],
+                        rhs=rc[a][:, v].bitcast(E4M3X4),
+                        rhs_scale=rs[a][:, v],
+                        start=(a == 0),
+                        stop=(a == NA - 1),
+                    )
+            return st
+
+        def h_out(g, q, st):
+            nc.vector.tensor_tensor(
+                out=hg[g][:, 512 * q : 512 * (q + 1)].rearrange("p (v t) -> p v t", t=4),
+                in0=st[:].rearrange("p t v -> p v t"),
+                in1=d1[:, g, :].unsqueeze(1).to_broadcast([P, P, 4]),
+                op=MULT,
+            )
+
+        acc = {}
+
+        def stage2(j, g):
+            nc.tensor.matmul_mx(
+                out=acc[j][:],
+                lhsT=cw[g][:, 256 * j : 256 * (j + 1)].bitcast(E2M1X4),
+                lhsT_scale=cs[:, 2048 * g + P * j : 2048 * g + P * (j + 1)],
+                rhs=hc[g][:].bitcast(E4M3X4),
+                rhs_scale=hs[g][:],
+                start=(g == 0),
+                stop=(g == NG - 1),
+            )
+
+        def open_acc(j, b):
+            acc[j] = bank(b, [P, V], F32, "acc%d" % j)
+
+        def out_part(j, c0, c1, queue):
+            o = keep.tile([P, c1 - c0], F32, name="o%d_%d" % (j, c0), align_bytes=64)
+            nc.vector.scalar_tensor_tensor(
+                out=o[:],
+                in0=acc[j][:, c0:c1],
+                scalar=d2[:, j : j + 1],
+                in1=w[j // 4][:, j % 4, c0:c1],
+                op0=MULT,
+                op1=ADD,
+            )
+            queue.dma_start(out=out[P * j : P * (j + 1), c0:c1], in_=o[:])
+
+        pr = {}
+        pk = {}
+        sts = {}
+        hx = {}
+
+        def r_out(eng, a, h):
+            copy(eng, rg[a][:, 1024 * h : 1024 * (h + 1)], pr[a, h][:])
+
+        def h_out_s(g, q, st):
+            hx[g, q] = keep.tile([P, 4, P], BF16, name="hx%d%d" % (g, q), align_bytes=64)
+            for t in range(4):
+                nc.scalar.activation(out=hx[g, q][:, t, :], in_=st[:, t, :], func=COPY, scale=d1[:, g, t : t + 1])
+
+        def h_mix(g, q):
+            nc.vector.tensor_copy(
+                out=hg[g][:, 512 * q : 512 * (q + 1)].rearrange("p (v t) -> p v t", t=4),
+                in_=hx[g, q][:].rearrange("p t v -> p v t"),
+            )
+
+        wu = bank(0, [P, P], F32, "wu")
+        for i in range(24):
+            nc.tensor.matmul(out=wu[:], lhsT=ident[:], rhs=drow_z[:], start=True, stop=True)
+        pd = bank(1, [P, P], BF16, "pd")
+        nc.tensor.transpose(pd[:], drow[:], ident[:])
+        nc.vector.tensor_copy(out=d2[:], in_=pd[:, 0:NJ])
+        nc.vector.tensor_copy(out=d1[:], in_=d1raw[:])
+        widen("v", 0, 0)
+        widen("s", 0, 3)
+        widen("v", 0, 2)
+        widen("s", 1, 3)
+        widen("v", 0, 1)
+        widen("v", 1, 2)
+        pr[0, 1] = r_turn(0, 1, 0)
+        widen("v", 1, 1)
+        widen("v", 1, 0)
+        pr[0, 0] = r_turn(0, 0, 1)
+        r_out("s", 0, 1)
+        k_direct("v", 0, 0, 2, 4)
+        pr[1, 1] = r_turn(1, 1, 2)
+        r_out("s", 0, 0)
+        k_direct("v", 0, 0, 0, 2)
+        pr[1, 0] = r_turn(1, 0, 3)
+        r_out("s", 1, 1)
+        quant_r(0, 0)
+        pk[0, 1, 2] = k_turn(0, 1, 2, 4)
+        r_out("s", 1, 0)
+        quant_r(1, 1)
+        pk[0, 1, 0] = k_turn(0, 1, 0, 5)
+        quant_r(0, 1)
+        k_out("s", 0, 1, 2, pk[0, 1, 2])
+        quant_r(1, 0)
+        pk[1, 0, 2] = k_turn(1, 0, 2, 6)
+        quant_k(0, 0)
+        k_out("s", 0, 1, 0, pk[0, 1, 0])
+        pk[1, 0, 0] = k_turn(1, 0, 0, 7)
+        k_out("s", 1, 0, 2, pk[1, 0, 2])
+        quant_k(0, 1)
+        pk[1, 1, 2] = k_turn(1, 1, 2, 0)
+        k_out("s", 1, 0, 0, pk[1, 0, 0])
+        sts[0, 3] = stage1(0, 3, 1)
+        k_out("s", 1, 1, 2, pk[1, 1, 2])
+        quant_k(1, 0)
+        sts[0, 2] = stage1(0, 2, 2)
+        k_direct("s", 1, 1, 0, 2)
+        h_out(0, 3, sts[0, 3])
+        sts[0, 1] = stage1(0, 1, 3)
+        h_out(0, 2, sts[0, 2])
+        sts[0, 0] = stage1(0, 0, 4)
+        k_direct("s", 2, 1, 0, 2)
+        h_out(0, 1, sts[0, 1])
+        pk[2, 0, 2] = k_turn(2, 0, 2, 5)
+        quant_k(1, 1)
+        pk[3, 0, 2] = k_turn(3, 0, 2, 6)
+        h_out(0, 0, sts[0, 0])
+        k_direct("s", 2, 1, 2, 4)
+        sts[1, 0] = stage1(1, 0, 7)
+        quant_h(0)
+        sts[1, 1] = stage1(1, 1, 0)
+        k_out("s", 2, 0, 2, pk[2, 0, 2])
+        h_out(1, 0, sts[1, 0])
+        sts[1, 3] = stage1(1, 3, 1)
+        k_direct("s", 2, 0, 0, 2)
+        h_out(1, 1, sts[1, 1])
+        sts[1, 2] = stage1(1, 2, 2)
+        h_out(1, 3, sts[1, 3])
+        open_acc(4, 3)
+        stage2(4, 0)
+        k_out("s", 3, 0, 2, pk[3, 0, 2])
+        quant_k(2, 0)
+        open_acc(5, 4)
+        stage2(5, 0)
+        open_acc(7, 5)
+        stage2(7, 0)
+        k_direct("s", 3, 1, 2, 4)
+        quant_k(2, 1)
+        open_acc(0, 7)
+        stage2(0, 0)
+        open_acc(2, 0)
+        stage2(2, 0)
+        h_out(1, 2, sts[1, 2])
+        open_acc(14, 1)
+        stage2(14, 0)
+        sts[2, 3] = stage1(2, 3, 6)
+        k_direct("s", 3, 1, 0, 2)
+        quant_h(1)
+        sts[2, 2] = stage1(2, 2, 2)
+        h_out(2, 3, sts[2, 3])
+        stage2(5, 1)
+        k_direct("s", 3, 0, 0, 2)
+        stage2(14, 1)
+        quant_k(3, 1)
+        stage2(2, 1)
+        stage2(7, 1)
+        h_out(2, 2, sts[2, 2])
+        sts[2, 1] = stage1(2, 1, 6)
+        quant_k(3, 0)
+        sts[2, 0] = stage1(2, 0, 2)
+        h_out(2, 1, sts[2, 1])
+        stage2(0, 1)
+        stage2(4, 1)
+        h_out(2, 0, sts[2, 0])
+        sts[3, 2] = stage1(3, 2, 6)
+        quant_h(2)
+        sts[3, 0] = stage1(3, 0, 2)
+        h_out_s(3, 2, sts[3, 2])
+        stage2(2, 2)
+        h_out(3, 0, sts[3, 0])
+        stage2(5, 2)
+        stage2(7, 2)
+        h_mix(3, 2)
+        sts[3, 1] = stage1(3, 1, 6)
+        sts[3, 3] = stage1(3, 3, 2)
+        h_out_s(3, 1, sts[3, 1])
+        stage2(0, 2)
+        stage2(4, 2)
+        h_out_s(3, 3, sts[3, 3])
+        h_mix(3, 1)
+        open_acc(6, 6)
+        stage2(6, 0)
+        stage2(6, 1)
+        stage2(6, 2)
+        h_mix(3, 3)
+        open_acc(10, 2)
+        stage2(10, 0)
+        stage2(10, 1)
+        quant_h(3)
+        stage2(10, 2)
+        stage2(14, 2)
+        stage2(4, 3)
+        stage2(2, 3)
+        out_part(4, 0, V, nc.sync)
+        stage2(0, 3)
+        stage2(5, 3)
+        out_part(0, 0, V, nc.sync)
+        stage2(6, 3)
+        stage2(10, 3)
+        out_part(5, 0, V, nc.scalar)
+        stage2(14, 3)
+        open_acc(13, 3)
+        stage2(13, 0)
+        out_part(10, 0, V, nc.sync)
+        open_acc(1, 7)
+        stage2(1, 0)
+        stage2(1, 1)
+        out_part(2, 0, V, nc.sync)
+        open_acc(3, 4)
+        stage2(3, 0)
+        stage2(3, 1)
+        out_part(6, 0, V, nc.sync)
+        stage2(3, 2)
+        open_acc(11, 2)
+        stage2(11, 0)
+        out_part(14, 0, V, nc.sync)
+        stage2(13, 1)
+        stage2(13, 2)
+        open_acc(15, 0)
+        stage2(15, 0)
+        stage2(15, 1)
+        stage2(1, 2)
+        stage2(1, 3)
+        stage2(11, 1)
+        out_part(1, 0, V, nc.scalar)
+        stage2(11, 2)
+        stage2(13, 3)
+        stage2(7, 3)
+        out_part(13, 0, V, nc.scalar)
+        open_acc(12, 6)
+        stage2(12, 0)
+        stage2(3, 3)
+        out_part(7, 0, V, nc.scalar)
+        stage2(12, 1)
+        stage2(12, 2)
+        out_part(3, 0, V, nc.scalar)
+        stage2(12, 3)
+        stage2(11, 3)
+        out_part(12, 0, V, nc.sync)
+        stage2(15, 2)
+        stage2(15, 3)
+        out_part(11, 0, V, nc.scalar)
+        open_acc(8, 1)
+        stage2(8, 0)
+        stage2(8, 1)
+        out_part(15, 0, V, nc.scalar)
+        stage2(8, 2)
+        stage2(8, 3)
+        open_acc(9, 7)
+        stage2(9, 0)
+        out_part(8, 0, V, nc.sync)
+        stage2(9, 1)
+        stage2(9, 2)
+        stage2(9, 3)
+        out_part(9, 0, V // 2, nc.sync)
+        out_part(9, V // 2, V, nc.scalar)

@@ -57,22 +57,20 @@ def tile_memit_weight_edit_s13_kernel(
         d1raw = sb([P, NG, 4], BF16, "d1raw")
         d1 = sb([P, NG, 4], F32, "d1")
         drow = sb([P, P], BF16, "drow")
-        drow_z = sb([P, P], BF16, "drow_z")
         d2 = sb([P, NJ], F32, "d2")
         tiny = sb([P, 1], F32, "tiny")
         tiny2 = sb([P, 1], F32, "tiny2")
 
         ctx.enter_context(tc.manual_schedule())
 
+        nc.gpsimd.memset(drow[:], 0.0)
         nc.gpsimd.memset(tiny[:], 0.0)
         make_identity(nc, ident[:])
-        nc.gpsimd.memset(drow[:], 0.0)
-        nc.gpsimd.memset(drow_z[:], 0.0)
         nc.gpsimd.memset(cs[:].bitcast(I32), 0)
         nc.scalar.dma_start(out=rscale[:], in_=resid_scale.rearrange("(a p t) o -> p a (t o)", a=NA, t=4))
-        nc.scalar.activation(out=tiny2[:], in_=tiny[:], func=COPY)
         nc.scalar.dma_start(out=d1raw[:], in_=inv_std.rearrange("(g p t) -> p g t", g=NG, t=4))
         nc.scalar.dma_start(out=drow[0:NJ, :], in_=inv_std.rearrange("(j p) -> j p", p=P))
+        nc.scalar.activation(out=tiny2[:], in_=tiny[:], func=COPY)
 
         r8_in = resid_bytes.rearrange("(a p t) n -> a p t n", a=NA, t=4)
         keys_in = keys.rearrange("(a p t) i -> a p t i", a=NA, t=4)
@@ -115,33 +113,12 @@ def tile_memit_weight_edit_s13_kernel(
             else:
                 nc.scalar.copy(out=dst, in_=src)
 
-        def r_turn(a, h, b):
-            ps = bank(b, [P, 1024], BF16, "pr%d%d" % (a, h))
-            for u in range(2):
-                n0 = 256 * h + 128 * u
-                nc.tensor.matmul(
-                    out=ps[:, 512 * u : 512 * (u + 1)].rearrange("p (n t) -> p n t", t=4),
-                    lhsT=ident[:],
-                    rhs=rw[a][:, :, n0 : n0 + 128].rearrange("p t n -> p n t"),
-                    start=True,
-                    stop=True,
-                )
-            return ps
+        def r_direct(eng, a, h):
+            c = slice(256 * h, 256 * (h + 1))
+            copy(eng, rg[a][:, 1024 * h : 1024 * (h + 1)].rearrange("p (n t) -> p n t", t=4), rw[a][:, :, c].rearrange("p t n -> p n t"))
 
         def k_view(g, a, t0, t1):
             return raw[g][a][:].rearrange("p j (m t) -> p t m j", t=4)[:, t0:t1]
-
-        def k_turn(g, a, t0, b):
-            ps = bank(b, [P, 1024], BF16, "pk%d%d%d" % (g, a, t0))
-            for u in range(2):
-                nc.tensor.matmul(
-                    out=ps[:, 512 * u : 512 * (u + 1)].rearrange("p (m j) -> p m j", j=4),
-                    lhsT=ident[:],
-                    rhs=raw[g][a][:].rearrange("p j (m t) -> p t m j", t=4)[:, t0 + u],
-                    start=True,
-                    stop=True,
-                )
-            return ps
 
         def k_direct(eng, g, a, t0, t1):
             copy(
@@ -149,9 +126,6 @@ def tile_memit_weight_edit_s13_kernel(
                 grp[g][a][:, 512 * t0 : 512 * t1].rearrange("p (t m j) -> p t m j", m=128, j=4),
                 k_view(g, a, t0, t1),
             )
-
-        def k_out(eng, g, a, t0, ps):
-            copy(eng, grp[g][a][:, 512 * t0 : 512 * t0 + 1024], ps[:])
 
         def quant(codes, scales, src, c=slice(0, 512)):
             nc.vector.quantize_mx(
@@ -220,18 +194,15 @@ def tile_memit_weight_edit_s13_kernel(
             )
             queue.dma_start(out=out[P * j : P * (j + 1), c0:c1], in_=o[:])
 
-        pr = {}
-        pk = {}
         sts = {}
         hx = {}
 
-        def r_out(eng, a, h):
-            copy(eng, rg[a][:, 1024 * h : 1024 * (h + 1)], pr[a, h][:])
-
-        def h_out_s(g, q, st):
+        def h_out_s(g, q):
             hx[g, q] = keep.tile([P, 4, P], BF16, name="hx%d%d" % (g, q), align_bytes=64)
             for t in range(4):
-                nc.scalar.activation(out=hx[g, q][:, t, :], in_=st[:, t, :], func=COPY, scale=d1[:, g, t : t + 1])
+                nc.scalar.activation(
+                    out=hx[g, q][:, t, :], in_=sts[g, q][:, t, :], func=COPY, scale=d1[:, g, t : t + 1]
+                )
 
         def h_mix(g, q):
             nc.vector.tensor_copy(
@@ -239,197 +210,111 @@ def tile_memit_weight_edit_s13_kernel(
                 in_=hx[g, q][:].rearrange("p t v -> p v t"),
             )
 
-        wu = bank(0, [P, P], F32, "wu")
-        for i in range(24):
-            nc.tensor.matmul(out=wu[:], lhsT=ident[:], rhs=drow_z[:], start=True, stop=True)
-        pd = bank(1, [P, P], BF16, "pd")
-        nc.tensor.transpose(pd[:], drow[:], ident[:])
-        nc.vector.tensor_copy(out=d2[:], in_=pd[:, 0:NJ])
-        nc.vector.tensor_copy(out=d1[:], in_=d1raw[:])
-        widen("v", 0, 0)
-        widen("s", 0, 3)
-        widen("v", 0, 2)
-        widen("s", 1, 3)
-        widen("v", 0, 1)
-        widen("v", 1, 2)
-        pr[0, 1] = r_turn(0, 1, 0)
-        widen("v", 1, 1)
-        widen("v", 1, 0)
-        pr[0, 0] = r_turn(0, 0, 1)
-        r_out("s", 0, 1)
-        k_direct("v", 0, 0, 2, 4)
-        pr[1, 1] = r_turn(1, 1, 2)
-        r_out("s", 0, 0)
-        k_direct("v", 0, 0, 0, 2)
-        pr[1, 0] = r_turn(1, 0, 3)
-        r_out("s", 1, 1)
+        def s1(g, q):
+            sts[g, q] = stage1(g, q, (4 * g + q) % 3)
+
+        def ev(g, q):
+            h_out(g, q, sts[g, q])
+
+        def passes(tiles, g):
+            for j in tiles:
+                stage2(j, g)
+
+        for a in range(NA):
+            for t in range(3):
+                widen("v", a, t)
+            widen("s", a, 3)
+        k_direct("s", 0, 0, 0, 2)
+        k_direct("s", 0, 0, 2, 4)
+        k_direct("s", 0, 1, 0, 2)
+        r_direct("v", 0, 0)
+        r_direct("v", 1, 0)
         quant_r(0, 0)
-        pk[0, 1, 2] = k_turn(0, 1, 2, 4)
-        r_out("s", 1, 0)
-        quant_r(1, 1)
-        pk[0, 1, 0] = k_turn(0, 1, 0, 5)
-        quant_r(0, 1)
-        k_out("s", 0, 1, 2, pk[0, 1, 2])
         quant_r(1, 0)
-        pk[1, 0, 2] = k_turn(1, 0, 2, 6)
+        k_direct("v", 0, 1, 2, 4)
         quant_k(0, 0)
-        k_out("s", 0, 1, 0, pk[0, 1, 0])
-        pk[1, 0, 0] = k_turn(1, 0, 0, 7)
-        k_out("s", 1, 0, 2, pk[1, 0, 2])
         quant_k(0, 1)
-        pk[1, 1, 2] = k_turn(1, 1, 2, 0)
-        k_out("s", 1, 0, 0, pk[1, 0, 0])
-        sts[0, 3] = stage1(0, 3, 1)
-        k_out("s", 1, 1, 2, pk[1, 1, 2])
-        quant_k(1, 0)
-        sts[0, 2] = stage1(0, 2, 2)
+        pd = bank(3, [P, P], BF16, "pd")
+        nc.tensor.transpose(pd[:], drow[:], ident[:])
+        nc.vector.tensor_copy(out=d1[:], in_=d1raw[:])
+        k_direct("s", 1, 0, 0, 2)
+        k_direct("s", 1, 0, 2, 4)
         k_direct("s", 1, 1, 0, 2)
-        h_out(0, 3, sts[0, 3])
-        sts[0, 1] = stage1(0, 1, 3)
-        h_out(0, 2, sts[0, 2])
-        sts[0, 0] = stage1(0, 0, 4)
-        k_direct("s", 2, 1, 0, 2)
-        h_out(0, 1, sts[0, 1])
-        pk[2, 0, 2] = k_turn(2, 0, 2, 5)
+        s1(0, 0)
+        s1(0, 1)
+        r_direct("v", 0, 1)
+        r_direct("v", 1, 1)
+        ev(0, 0)
+        quant_r(0, 1)
+        quant_r(1, 1)
+        ev(0, 1)
+        nc.vector.tensor_copy(out=d2[:], in_=pd[:, 0:NJ])
+        s1(0, 2)
+        s1(0, 3)
+        k_direct("v", 1, 1, 2, 4)
+        quant_k(1, 0)
+        ev(0, 2)
         quant_k(1, 1)
-        pk[3, 0, 2] = k_turn(3, 0, 2, 6)
-        h_out(0, 0, sts[0, 0])
-        k_direct("s", 2, 1, 2, 4)
-        sts[1, 0] = stage1(1, 0, 7)
+        for a in range(NA):
+            k_direct("s", 2, a, 0, 2)
+            k_direct("s", 2, a, 2, 4)
+        s1(1, 0)
+        ev(0, 3)
         quant_h(0)
-        sts[1, 1] = stage1(1, 1, 0)
-        k_out("s", 2, 0, 2, pk[2, 0, 2])
-        h_out(1, 0, sts[1, 0])
-        sts[1, 3] = stage1(1, 3, 1)
-        k_direct("s", 2, 0, 0, 2)
-        h_out(1, 1, sts[1, 1])
-        sts[1, 2] = stage1(1, 2, 2)
-        h_out(1, 3, sts[1, 3])
-        open_acc(4, 3)
-        stage2(4, 0)
-        k_out("s", 3, 0, 2, pk[3, 0, 2])
+        s1(1, 1)
+        s1(1, 2)
+        ev(1, 0)
+        s1(1, 3)
+        ev(1, 1)
+        ev(1, 2)
         quant_k(2, 0)
-        open_acc(5, 4)
-        stage2(5, 0)
-        open_acc(7, 5)
-        stage2(7, 0)
-        k_direct("s", 3, 1, 2, 4)
         quant_k(2, 1)
-        open_acc(0, 7)
-        stage2(0, 0)
-        open_acc(2, 0)
-        stage2(2, 0)
-        h_out(1, 2, sts[1, 2])
-        open_acc(14, 1)
-        stage2(14, 0)
-        sts[2, 3] = stage1(2, 3, 6)
-        k_direct("s", 3, 1, 0, 2)
+        for a in range(NA):
+            k_direct("s", 3, a, 0, 2)
+            k_direct("s", 3, a, 2, 4)
+        for j in range(5):
+            open_acc(j, 3 + j)
+        passes(range(5), 0)
+        s1(2, 0)
+        ev(1, 3)
         quant_h(1)
-        sts[2, 2] = stage1(2, 2, 2)
-        h_out(2, 3, sts[2, 3])
-        stage2(5, 1)
-        k_direct("s", 3, 0, 0, 2)
-        stage2(14, 1)
-        quant_k(3, 1)
-        stage2(2, 1)
-        stage2(7, 1)
-        h_out(2, 2, sts[2, 2])
-        sts[2, 1] = stage1(2, 1, 6)
+        s1(2, 1)
+        s1(2, 2)
+        ev(2, 0)
+        s1(2, 3)
+        ev(2, 1)
+        ev(2, 2)
+        passes(range(5), 1)
         quant_k(3, 0)
-        sts[2, 0] = stage1(2, 0, 2)
-        h_out(2, 1, sts[2, 1])
-        stage2(0, 1)
-        stage2(4, 1)
-        h_out(2, 0, sts[2, 0])
-        sts[3, 2] = stage1(3, 2, 6)
+        quant_k(3, 1)
+        s1(3, 0)
+        ev(2, 3)
         quant_h(2)
-        sts[3, 0] = stage1(3, 0, 2)
-        h_out_s(3, 2, sts[3, 2])
-        stage2(2, 2)
-        h_out(3, 0, sts[3, 0])
-        stage2(5, 2)
-        stage2(7, 2)
-        h_mix(3, 2)
-        sts[3, 1] = stage1(3, 1, 6)
-        sts[3, 3] = stage1(3, 3, 2)
-        h_out_s(3, 1, sts[3, 1])
-        stage2(0, 2)
-        stage2(4, 2)
-        h_out_s(3, 3, sts[3, 3])
+        s1(3, 1)
+        s1(3, 2)
+        ev(3, 0)
+        s1(3, 3)
+        h_out_s(3, 1)
+        ev(3, 2)
+        h_out_s(3, 3)
         h_mix(3, 1)
-        open_acc(6, 6)
-        stage2(6, 0)
-        stage2(6, 1)
-        stage2(6, 2)
         h_mix(3, 3)
-        open_acc(10, 2)
-        stage2(10, 0)
-        stage2(10, 1)
+        passes(range(5), 2)
+        bank_of = [3, 4, 5, 6, 7, 1, 2, 0]
+        for j in range(5, 8):
+            open_acc(j, bank_of[j])
+            for g in range(3):
+                stage2(j, g)
         quant_h(3)
-        stage2(10, 2)
-        stage2(14, 2)
-        stage2(4, 3)
-        stage2(2, 3)
-        out_part(4, 0, V, nc.sync)
-        stage2(0, 3)
-        stage2(5, 3)
-        out_part(0, 0, V, nc.sync)
-        stage2(6, 3)
-        stage2(10, 3)
-        out_part(5, 0, V, nc.scalar)
-        stage2(14, 3)
-        open_acc(13, 3)
-        stage2(13, 0)
-        out_part(10, 0, V, nc.sync)
-        open_acc(1, 7)
-        stage2(1, 0)
-        stage2(1, 1)
-        out_part(2, 0, V, nc.sync)
-        open_acc(3, 4)
-        stage2(3, 0)
-        stage2(3, 1)
-        out_part(6, 0, V, nc.sync)
-        stage2(3, 2)
-        open_acc(11, 2)
-        stage2(11, 0)
-        out_part(14, 0, V, nc.sync)
-        stage2(13, 1)
-        stage2(13, 2)
-        open_acc(15, 0)
-        stage2(15, 0)
-        stage2(15, 1)
-        stage2(1, 2)
-        stage2(1, 3)
-        stage2(11, 1)
-        out_part(1, 0, V, nc.scalar)
-        stage2(11, 2)
-        stage2(13, 3)
-        stage2(7, 3)
-        out_part(13, 0, V, nc.scalar)
-        open_acc(12, 6)
-        stage2(12, 0)
-        stage2(3, 3)
-        out_part(7, 0, V, nc.scalar)
-        stage2(12, 1)
-        stage2(12, 2)
-        out_part(3, 0, V, nc.scalar)
-        stage2(12, 3)
-        stage2(11, 3)
-        out_part(12, 0, V, nc.sync)
-        stage2(15, 2)
-        stage2(15, 3)
-        out_part(11, 0, V, nc.scalar)
-        open_acc(8, 1)
-        stage2(8, 0)
-        stage2(8, 1)
-        out_part(15, 0, V, nc.scalar)
-        stage2(8, 2)
-        stage2(8, 3)
-        open_acc(9, 7)
-        stage2(9, 0)
-        out_part(8, 0, V, nc.sync)
-        stage2(9, 1)
-        stage2(9, 2)
-        stage2(9, 3)
-        out_part(9, 0, V // 2, nc.sync)
-        out_part(9, V // 2, V, nc.scalar)
+        for j in range(8):
+            stage2(j, 3)
+            out_part(j, 0, V, nc.sync if j % 2 == 0 else nc.scalar)
+        for j in range(8, NJ):
+            open_acc(j, bank_of[j - 8])
+            for g in range(NG):
+                stage2(j, g)
+            if j < NJ - 1:
+                out_part(j, 0, V, nc.sync if j % 2 == 0 else nc.scalar)
+            else:
+                out_part(j, 0, V // 2, nc.sync)
+                out_part(j, V // 2, V, nc.scalar)

@@ -37,7 +37,8 @@ def tile_memit_weight_edit_s13_kernel(
         def bank(i, shape, dtype, name):
             return psum.tile(shape, dtype, name=name, tag="bank%d" % i)
 
-        raw = [[sb([P, 4, 512], BF16, "raw%d%d" % (g, a)) for a in range(NA)] for g in range(NG)]
+        raw = [[sb([P, 4, 512], BF16, "raw%d%d" % (g, a)) for a in range(NA)] for g in range(2)]
+        raw_b = [sb([P, 4, 1024], BF16, "rawb%d" % a) for a in range(NA)]
         grp = [[sb([P, 2048], BF16, "grp%d%d" % (g, a)) for a in range(NA)] for g in range(NG)]
         kc = [[sb([P, 512], U32, "kc%d%d" % (g, a)) for a in range(NA)] for g in range(NG)]
         ks = [[sb([P, 512], U8, "ks%d%d" % (g, a)) for a in range(NA)] for g in range(NG)]
@@ -86,8 +87,8 @@ def tile_memit_weight_edit_s13_kernel(
             nc.sync.dma_start(out=r8[a][:], in_=r8_in[a])
         load_keys(0)
         load_keys(1)
-        load_keys(2)
-        load_keys(3)
+        for a in range(NA):
+            nc.sync.dma_start(out=raw_b[a][:], in_=keys_in[a][:, :, 1024:2048])
         for q in range(4):
             nc.sync.dma_start(
                 out=cs_w[32 * q : 32 * q + 4, :].rearrange("p (g n) -> p g n", g=NG),
@@ -114,17 +115,20 @@ def tile_memit_weight_edit_s13_kernel(
                 nc.scalar.copy(out=dst, in_=src)
 
         def r_direct(eng, a, h):
-            c = slice(256 * h, 256 * (h + 1))
-            copy(eng, rg[a][:, 1024 * h : 1024 * (h + 1)].rearrange("p (n t) -> p n t", t=4), rw[a][:, :, c].rearrange("p t n -> p n t"))
-
-        def k_view(g, a, t0, t1):
-            return raw[g][a][:].rearrange("p j (m t) -> p t m j", t=4)[:, t0:t1]
-
-        def k_direct(eng, g, a, t0, t1):
             copy(
                 eng,
-                grp[g][a][:, 512 * t0 : 512 * t1].rearrange("p (t m j) -> p t m j", m=128, j=4),
-                k_view(g, a, t0, t1),
+                rg[a][:, 1024 * h : 1024 * (h + 1)].rearrange("p (c i t) -> p c t i", i=4, t=4),
+                rw[a][:, :, 256 * h : 256 * (h + 1)].rearrange("p t (c i) -> p c t i", i=4),
+            )
+
+        def k_rows(g, a):
+            return raw[g][a][:] if g < 2 else raw_b[a][:, :, 512 * (g - 2) : 512 * (g - 1)]
+
+        def k_direct(eng, g, a, m0, m1):
+            copy(
+                eng,
+                grp[g][a][:].rearrange("p (t m j) -> p m j t", t=4, j=4)[:, m0:m1],
+                k_rows(g, a).rearrange("p j (m t) -> p m j t", t=4)[:, m0:m1],
             )
 
         def quant(codes, scales, src, c=slice(0, 512)):
@@ -206,8 +210,8 @@ def tile_memit_weight_edit_s13_kernel(
 
         def h_mix(g, q):
             nc.vector.tensor_copy(
-                out=hg[g][:, 512 * q : 512 * (q + 1)].rearrange("p (v t) -> p v t", t=4),
-                in_=hx[g, q][:].rearrange("p t v -> p v t"),
+                out=hg[g][:, 512 * q : 512 * (q + 1)].rearrange("p (c i t) -> p c t i", i=4, t=4),
+                in_=hx[g, q][:].rearrange("p t (c i) -> p c t i", i=4),
             )
 
         def s1(g, q):
@@ -224,22 +228,22 @@ def tile_memit_weight_edit_s13_kernel(
             for t in range(3):
                 widen("v", a, t)
             widen("s", a, 3)
-        k_direct("s", 0, 0, 0, 2)
-        k_direct("s", 0, 0, 2, 4)
-        k_direct("s", 0, 1, 0, 2)
+        k_direct("s", 0, 0, 0, 64)
+        k_direct("s", 0, 0, 64, 128)
+        k_direct("s", 0, 1, 0, 64)
         r_direct("v", 0, 0)
         r_direct("v", 1, 0)
         quant_r(0, 0)
         quant_r(1, 0)
-        k_direct("v", 0, 1, 2, 4)
+        k_direct("v", 0, 1, 64, 128)
         quant_k(0, 0)
         quant_k(0, 1)
         pd = bank(3, [P, P], BF16, "pd")
         nc.tensor.transpose(pd[:], drow[:], ident[:])
         nc.vector.tensor_copy(out=d1[:], in_=d1raw[:])
-        k_direct("s", 1, 0, 0, 2)
-        k_direct("s", 1, 0, 2, 4)
-        k_direct("s", 1, 1, 0, 2)
+        k_direct("s", 1, 0, 0, 64)
+        k_direct("s", 1, 0, 64, 128)
+        k_direct("s", 1, 1, 0, 64)
         s1(0, 0)
         s1(0, 1)
         r_direct("v", 0, 1)
@@ -251,13 +255,13 @@ def tile_memit_weight_edit_s13_kernel(
         nc.vector.tensor_copy(out=d2[:], in_=pd[:, 0:NJ])
         s1(0, 2)
         s1(0, 3)
-        k_direct("v", 1, 1, 2, 4)
+        k_direct("v", 1, 1, 64, 128)
         quant_k(1, 0)
         ev(0, 2)
         quant_k(1, 1)
         for a in range(NA):
-            k_direct("s", 2, a, 0, 2)
-            k_direct("s", 2, a, 2, 4)
+            k_direct("s", 2, a, 0, 64)
+            k_direct("s", 2, a, 64, 128)
         s1(1, 0)
         ev(0, 3)
         quant_h(0)
@@ -270,8 +274,8 @@ def tile_memit_weight_edit_s13_kernel(
         quant_k(2, 0)
         quant_k(2, 1)
         for a in range(NA):
-            k_direct("s", 3, a, 0, 2)
-            k_direct("s", 3, a, 2, 4)
+            k_direct("s", 3, a, 0, 64)
+            k_direct("s", 3, a, 64, 128)
         for j in range(5):
             open_acc(j, 3 + j)
         passes(range(5), 0)

@@ -37,8 +37,7 @@ def tile_memit_weight_edit_s13_kernel(
         def bank(i, shape, dtype, name):
             return psum.tile(shape, dtype, name=name, tag="bank%d" % i)
 
-        raw = [[sb([P, 4, 512], BF16, "raw%d%d" % (g, a)) for a in range(NA)] for g in range(2)]
-        raw_b = [sb([P, 4, 1024], BF16, "rawb%d" % a) for a in range(NA)]
+        raw = [[sb([P, 4, 512], BF16, "raw%d%d" % (g, a)) for a in range(NA)] for g in range(NG)]
         grp = [[sb([P, 2048], BF16, "grp%d%d" % (g, a)) for a in range(NA)] for g in range(NG)]
         kc = [[sb([P, 512], U32, "kc%d%d" % (g, a)) for a in range(NA)] for g in range(NG)]
         ks = [[sb([P, 512], U8, "ks%d%d" % (g, a)) for a in range(NA)] for g in range(NG)]
@@ -55,7 +54,7 @@ def tile_memit_weight_edit_s13_kernel(
         w = [sb([P, 4, 512], BF16, "w%d" % i) for i in range(4)]
         ident = sb([P, P], BF16, "ident")
         rscale = sb([P, NA, 4], F32, "rscale")
-        d1raw = sb([P, NG, 4], BF16, "d1raw")
+        drow4 = sb([P, 512], BF16, "drow4")
         d1 = sb([P, NG, 4], F32, "d1")
         drow = sb([P, P], BF16, "drow")
         d2 = sb([P, NJ], F32, "d2")
@@ -65,12 +64,13 @@ def tile_memit_weight_edit_s13_kernel(
         ctx.enter_context(tc.manual_schedule())
 
         nc.gpsimd.memset(drow[:], 0.0)
+        nc.gpsimd.memset(drow4[:], 0.0)
         nc.gpsimd.memset(tiny[:], 0.0)
         make_identity(nc, ident[:])
         nc.gpsimd.memset(cs[:].bitcast(I32), 0)
         nc.scalar.dma_start(out=rscale[:], in_=resid_scale.rearrange("(a p t) o -> p a (t o)", a=NA, t=4))
-        nc.scalar.dma_start(out=d1raw[:], in_=inv_std.rearrange("(g p t) -> p g t", g=NG, t=4))
         nc.scalar.dma_start(out=drow[0:NJ, :], in_=inv_std.rearrange("(j p) -> j p", p=P))
+        nc.scalar.dma_start(out=drow4[0:NG, :], in_=inv_std.rearrange("(g c) -> g c", g=NG))
         nc.scalar.activation(out=tiny2[:], in_=tiny[:], func=COPY)
 
         r8_in = resid_bytes.rearrange("(a p t) n -> a p t n", a=NA, t=4)
@@ -83,19 +83,23 @@ def tile_memit_weight_edit_s13_kernel(
             for a in range(NA):
                 nc.sync.dma_start(out=raw[g][a][:], in_=keys_in[a][:, :, 512 * g : 512 * (g + 1)])
 
+        def load_scales(g):
+            for q in range(4):
+                nc.sync.dma_start(
+                    out=cs_w[32 * q : 32 * q + 4, 512 * g : 512 * (g + 2)].rearrange("p (g n) -> p g n", g=2),
+                    in_=cs_in[g : g + 2, 4 * q : 4 * q + 4, :].rearrange("g q n -> q g n"),
+                )
+
         for a in range(NA):
             nc.sync.dma_start(out=r8[a][:], in_=r8_in[a])
         load_keys(0)
         load_keys(1)
-        for a in range(NA):
-            nc.sync.dma_start(out=raw_b[a][:], in_=keys_in[a][:, :, 1024:2048])
-        for q in range(4):
-            nc.sync.dma_start(
-                out=cs_w[32 * q : 32 * q + 4, :].rearrange("p (g n) -> p g n", g=NG),
-                in_=cs_in[:, 4 * q : 4 * q + 4, :].rearrange("g q n -> q g n"),
-            )
+        load_keys(2)
+        load_scales(0)
         nc.sync.dma_start(out=cw[0][:], in_=cinv_words[0])
+        load_keys(3)
         nc.sync.dma_start(out=cw[1][:], in_=cinv_words[1])
+        load_scales(2)
         nc.sync.dma_start(out=cw[2][:], in_=cinv_words[2])
         nc.sync.dma_start(out=cw[3][:], in_=cinv_words[3])
         for i in range(4):
@@ -121,14 +125,11 @@ def tile_memit_weight_edit_s13_kernel(
                 rw[a][:, :, 256 * h : 256 * (h + 1)].rearrange("p t (c i) -> p c t i", i=4),
             )
 
-        def k_rows(g, a):
-            return raw[g][a][:] if g < 2 else raw_b[a][:, :, 512 * (g - 2) : 512 * (g - 1)]
-
         def k_direct(eng, g, a, m0, m1):
             copy(
                 eng,
                 grp[g][a][:].rearrange("p (t m j) -> p m j t", t=4, j=4)[:, m0:m1],
-                k_rows(g, a).rearrange("p j (m t) -> p m j t", t=4)[:, m0:m1],
+                raw[g][a][:].rearrange("p j (m t) -> p m j t", t=4)[:, m0:m1],
             )
 
         def quant(codes, scales, src, c=slice(0, 512)):
@@ -214,8 +215,10 @@ def tile_memit_weight_edit_s13_kernel(
                 in_=hx[g, q][:].rearrange("p t (c i) -> p c t i", i=4),
             )
 
+        stage1_bank = [[0, 1, 2, 3], [6, 7, 0, 1], [0, 1, 0, 1], [0, 1, 0, 1]]
+
         def s1(g, q):
-            sts[g, q] = stage1(g, q, (4 * g + q) % 3)
+            sts[g, q] = stage1(g, q, stage1_bank[g][q])
 
         def ev(g, q):
             h_out(g, q, sts[g, q])
@@ -224,6 +227,10 @@ def tile_memit_weight_edit_s13_kernel(
             for j in tiles:
                 stage2(j, g)
 
+        pd = bank(7, [P, 5, P], BF16, "pd")
+        nc.tensor.transpose(pd[:, 4, :], drow[:], ident[:])
+        for t in range(4):
+            nc.tensor.transpose(pd[:, t, :], drow4[:, t::4], ident[:])
         for a in range(NA):
             for t in range(3):
                 widen("v", a, t)
@@ -233,52 +240,50 @@ def tile_memit_weight_edit_s13_kernel(
         k_direct("s", 0, 1, 0, 64)
         r_direct("v", 0, 0)
         r_direct("v", 1, 0)
+        nc.vector.tensor_copy(out=d1[:], in_=pd[:, 0:4, 0:NG].rearrange("p t g -> p g t"))
+        nc.vector.tensor_copy(out=d2[:], in_=pd[:, 4, 0:NJ])
         quant_r(0, 0)
         quant_r(1, 0)
         k_direct("v", 0, 1, 64, 128)
         quant_k(0, 0)
         quant_k(0, 1)
-        pd = bank(3, [P, P], BF16, "pd")
-        nc.tensor.transpose(pd[:], drow[:], ident[:])
-        nc.vector.tensor_copy(out=d1[:], in_=d1raw[:])
         k_direct("s", 1, 0, 0, 64)
         k_direct("s", 1, 0, 64, 128)
         k_direct("s", 1, 1, 0, 64)
         s1(0, 0)
         s1(0, 1)
+        k_direct("v", 1, 1, 64, 128)
         r_direct("v", 0, 1)
         r_direct("v", 1, 1)
-        ev(0, 0)
         quant_r(0, 1)
         quant_r(1, 1)
-        ev(0, 1)
-        nc.vector.tensor_copy(out=d2[:], in_=pd[:, 0:NJ])
         s1(0, 2)
         s1(0, 3)
-        k_direct("v", 1, 1, 64, 128)
         quant_k(1, 0)
-        ev(0, 2)
         quant_k(1, 1)
+        s1(1, 0)
+        s1(1, 1)
         for a in range(NA):
             k_direct("s", 2, a, 0, 64)
             k_direct("s", 2, a, 64, 128)
-        s1(1, 0)
-        ev(0, 3)
-        quant_h(0)
-        s1(1, 1)
+        ev(0, 0)
         s1(1, 2)
-        ev(1, 0)
+        ev(0, 1)
         s1(1, 3)
+        ev(0, 2)
+        ev(0, 3)
+        ev(1, 0)
+        quant_h(0)
         ev(1, 1)
+        for j in range(6):
+            open_acc(j, 2 + j)
+        passes(range(6), 0)
         ev(1, 2)
         quant_k(2, 0)
         quant_k(2, 1)
         for a in range(NA):
             k_direct("s", 3, a, 0, 64)
             k_direct("s", 3, a, 64, 128)
-        for j in range(5):
-            open_acc(j, 3 + j)
-        passes(range(5), 0)
         s1(2, 0)
         ev(1, 3)
         quant_h(1)
@@ -288,7 +293,7 @@ def tile_memit_weight_edit_s13_kernel(
         s1(2, 3)
         ev(2, 1)
         ev(2, 2)
-        passes(range(5), 1)
+        passes(range(6), 1)
         quant_k(3, 0)
         quant_k(3, 1)
         s1(3, 0)
@@ -303,18 +308,17 @@ def tile_memit_weight_edit_s13_kernel(
         h_out_s(3, 3)
         h_mix(3, 1)
         h_mix(3, 3)
-        passes(range(5), 2)
-        bank_of = [3, 4, 5, 6, 7, 1, 2, 0]
-        for j in range(5, 8):
-            open_acc(j, bank_of[j])
-            for g in range(3):
-                stage2(j, g)
+        passes(range(6), 2)
+        bank_of = [2, 3, 4, 5, 6, 7, 0, 1]
+        open_acc(6, 0)
+        for g in range(3):
+            stage2(6, g)
         quant_h(3)
-        for j in range(8):
+        for j in range(7):
             stage2(j, 3)
             out_part(j, 0, V, nc.sync if j % 2 == 0 else nc.scalar)
-        for j in range(8, NJ):
-            open_acc(j, bank_of[j - 8])
+        for j in range(7, NJ):
+            open_acc(j, bank_of[j % 8])
             for g in range(NG):
                 stage2(j, g)
             if j < NJ - 1:

@@ -15,12 +15,22 @@ MULT = mybir.AluOpType.mult
 ADD = mybir.AluOpType.add
 COPY = mybir.ActivationFunctionType.Copy
 
-P = 128
 E, D, V = 1024, 2048, 512
-NA = E // 512
-NG = D // 512
-NJ = D // P
+P = 128
+PACK = 4
+PASS = P * PACK
+EDIT_PASSES = E // PASS
+CHUNKS = D // PASS
+OUT_TILES = D // P
+QUARTERS = V // P
+
 FLOPS = 2 * E * D * V + 2 * D * D * V
+
+SCALAR_KEYS = {(0, 1): 64, (1, 1): 64, (2, 1): 96}
+
+PRODUCT1_BANKS = [[0, 1, 2, 3], [6, 7, 0, 1], [0, 1, 0, 1], [0, 1, 0, 1]]
+EARLY_TILES = 6
+FIRST_TILE_BANK = 2
 
 
 def tile_memit_weight_edit_s13_kernel(
@@ -31,298 +41,281 @@ def tile_memit_weight_edit_s13_kernel(
         keep = ctx.enter_context(tc.tile_pool(name="keep", bufs=1))
         psum = ctx.enter_context(tc.psum_pool(name="psum", bufs=1))
 
-        def sb(shape, dtype, name):
+        def sbuf_tile(shape, dtype, name):
             return keep.tile(shape, dtype, name=name, align_bytes=64)
 
-        def bank(i, shape, dtype, name):
-            return psum.tile(shape, dtype, name=name, tag="bank%d" % i)
+        def bank_tile(bank, shape, dtype, name):
+            return psum.tile(shape, dtype, name=name, tag="bank%d" % bank)
 
-        raw = [[sb([P, 4, 512], BF16, "raw%d%d" % (g, a)) for a in range(NA)] for g in range(NG)]
-        grp = [[sb([P, 2048], BF16, "grp%d%d" % (g, a)) for a in range(NA)] for g in range(NG)]
-        kc = [[sb([P, 512], U32, "kc%d%d" % (g, a)) for a in range(NA)] for g in range(NG)]
-        ks = [[sb([P, 512], U8, "ks%d%d" % (g, a)) for a in range(NA)] for g in range(NG)]
-        r8 = [sb([P, 4, 512], U8, "r8%d" % a) for a in range(NA)]
-        rw = [sb([P, 4, 512], BF16, "rw%d" % a) for a in range(NA)]
-        rg = [sb([P, 2048], BF16, "rg%d" % a) for a in range(NA)]
-        rc = [sb([P, 512], U32, "rc%d" % a) for a in range(NA)]
-        rs = [sb([P, 512], U8, "rs%d" % a) for a in range(NA)]
-        hg = [sb([P, 2048], BF16, "hg%d" % g) for g in range(NG)]
-        hc = [sb([P, 512], U32, "hc%d" % g) for g in range(NG)]
-        hs = [sb([P, 512], U8, "hs%d" % g) for g in range(NG)]
-        cw = [sb([P, 4096], U8, "cw%d" % g) for g in range(NG)]
-        cs = sb([P, NG * 2048], U8, "cs")
-        w = [sb([P, 4, 512], BF16, "w%d" % i) for i in range(4)]
-        ident = sb([P, P], BF16, "ident")
-        rscale = sb([P, NA, 4], F32, "rscale")
-        drow4 = sb([P, 512], BF16, "drow4")
-        d1 = sb([P, NG, 4], F32, "d1")
-        drow = sb([P, P], BF16, "drow")
-        d2 = sb([P, NJ], F32, "d2")
-        tiny = sb([P, 1], F32, "tiny")
-        tiny2 = sb([P, 1], F32, "tiny2")
+        def per_keys(shape, dtype, name):
+            return [
+                [sbuf_tile(shape, dtype, "%s%d%d" % (name, g, a)) for a in range(EDIT_PASSES)] for g in range(CHUNKS)
+            ]
+
+        keys_raw = per_keys([P, PACK, PASS], BF16, "keys_raw")
+        keys_mix = per_keys([P, PACK * PASS], BF16, "keys_mix")
+        keys_codes = per_keys([P, PASS], U32, "keys_codes")
+        keys_scales = per_keys([P, PASS], U8, "keys_scales")
+        resid_b = [sbuf_tile([P, PACK, V], U8, "resid_b%d" % a) for a in range(EDIT_PASSES)]
+        resid_w = [sbuf_tile([P, PACK, V], BF16, "resid_w%d" % a) for a in range(EDIT_PASSES)]
+        resid_mix = [sbuf_tile([P, PACK * V], BF16, "resid_mix%d" % a) for a in range(EDIT_PASSES)]
+        resid_codes = [sbuf_tile([P, V], U32, "resid_codes%d" % a) for a in range(EDIT_PASSES)]
+        resid_scales = [sbuf_tile([P, V], U8, "resid_scales%d" % a) for a in range(EDIT_PASSES)]
+        h_mix = [sbuf_tile([P, PACK * V], BF16, "h_mix%d" % g) for g in range(CHUNKS)]
+        h_codes = [sbuf_tile([P, V], U32, "h_codes%d" % g) for g in range(CHUNKS)]
+        h_scales = [sbuf_tile([P, V], U8, "h_scales%d" % g) for g in range(CHUNKS)]
+        c_words = [sbuf_tile([P, 2 * D], U8, "c_words%d" % g) for g in range(CHUNKS)]
+        c_scales = sbuf_tile([P, CHUNKS * D], U8, "c_scales")
+        w_rows = [sbuf_tile([P, 4, V], BF16, "w_rows%d" % b) for b in range(OUT_TILES // 4)]
+        ident = sbuf_tile([P, P], BF16, "ident")
+        edit_scale = sbuf_tile([P, EDIT_PASSES, PACK], F32, "edit_scale")
+        inv_rows = sbuf_tile([P, P + PASS], BF16, "inv_rows")
+        inv_in = sbuf_tile([P, CHUNKS, PACK], F32, "inv_in")
+        inv_out = sbuf_tile([P, OUT_TILES], F32, "inv_out")
+        zero = sbuf_tile([P, 1], F32, "zero")
+        warm = sbuf_tile([P, 1], F32, "warm")
 
         ctx.enter_context(tc.manual_schedule())
 
-        nc.gpsimd.memset(drow[:], 0.0)
-        nc.gpsimd.memset(drow4[:], 0.0)
-        nc.gpsimd.memset(tiny[:], 0.0)
+        nc.gpsimd.memset(inv_rows[:], 0.0)
+        nc.gpsimd.memset(zero[:], 0.0)
         make_identity(nc, ident[:])
-        nc.gpsimd.memset(cs[:].bitcast(I32), 0)
-        nc.scalar.dma_start(out=rscale[:], in_=resid_scale.rearrange("(a p t) o -> p a (t o)", a=NA, t=4))
-        nc.scalar.dma_start(out=drow[0:NJ, :], in_=inv_std.rearrange("(j p) -> j p", p=P))
-        nc.scalar.dma_start(out=drow4[0:NG, :], in_=inv_std.rearrange("(g c) -> g c", g=NG))
-        nc.scalar.activation(out=tiny2[:], in_=tiny[:], func=COPY)
+        nc.gpsimd.memset(c_scales[:].bitcast(I32), 0)
+        nc.scalar.dma_start(out=edit_scale[:], in_=resid_scale.rearrange("(a p t) o -> p a (t o)", a=EDIT_PASSES, t=PACK))
+        nc.scalar.dma_start(out=inv_rows[0:OUT_TILES, 0:P], in_=inv_std.rearrange("(j p) -> j p", p=P))
+        nc.scalar.dma_start(out=inv_rows[0:CHUNKS, P:], in_=inv_std.rearrange("(g c) -> g c", g=CHUNKS))
+        nc.scalar.activation(out=warm[:], in_=zero[:], func=COPY)
 
-        r8_in = resid_bytes.rearrange("(a p t) n -> a p t n", a=NA, t=4)
-        keys_in = keys.rearrange("(a p t) i -> a p t i", a=NA, t=4)
+        keys_in = keys.rearrange("(a p t) i -> a p t i", a=EDIT_PASSES, t=PACK)
+        resid_in = resid_bytes.rearrange("(a p t) v -> a p t v", a=EDIT_PASSES, t=PACK)
         w_in = w_old.rearrange("(b q p) v -> b p q v", q=4, p=P)
-        cs_in = cinv_scales.bitcast(I32)
-        cs_w = cs[:].bitcast(I32)
+        c_scales_in = cinv_scales.bitcast(I32)
+        c_scales_words = c_scales[:].bitcast(I32)
 
         def load_keys(g):
-            for a in range(NA):
-                nc.sync.dma_start(out=raw[g][a][:], in_=keys_in[a][:, :, 512 * g : 512 * (g + 1)])
+            for a in range(EDIT_PASSES):
+                nc.sync.dma_start(out=keys_raw[g][a][:], in_=keys_in[a][:, :, PASS * g : PASS * (g + 1)])
 
-        def load_scales(g):
+        def load_c_scales(g):
             for q in range(4):
                 nc.sync.dma_start(
-                    out=cs_w[32 * q : 32 * q + 4, 512 * g : 512 * (g + 2)].rearrange("p (g n) -> p g n", g=2),
-                    in_=cs_in[g : g + 2, 4 * q : 4 * q + 4, :].rearrange("g q n -> q g n"),
+                    out=c_scales_words[32 * q : 32 * q + 4, 512 * g : 512 * (g + 2)].rearrange("p (g n) -> p g n", g=2),
+                    in_=c_scales_in[g : g + 2, 4 * q : 4 * q + 4, :].rearrange("g q n -> q g n"),
                 )
 
-        for a in range(NA):
-            nc.sync.dma_start(out=r8[a][:], in_=r8_in[a])
+        def load_c_words(g):
+            nc.sync.dma_start(out=c_words[g][:], in_=cinv_words[g])
+
+        for a in range(EDIT_PASSES):
+            nc.sync.dma_start(out=resid_b[a][:], in_=resid_in[a])
         load_keys(0)
         load_keys(1)
         load_keys(2)
-        load_scales(0)
-        nc.sync.dma_start(out=cw[0][:], in_=cinv_words[0])
+        load_c_scales(0)
+        load_c_words(0)
         load_keys(3)
-        nc.sync.dma_start(out=cw[1][:], in_=cinv_words[1])
-        load_scales(2)
-        nc.sync.dma_start(out=cw[2][:], in_=cinv_words[2])
-        nc.sync.dma_start(out=cw[3][:], in_=cinv_words[3])
-        for i in range(4):
-            nc.sync.dma_start(out=w[i][:], in_=w_in[i])
+        load_c_words(1)
+        load_c_scales(2)
+        load_c_words(2)
+        load_c_words(3)
+        for b in range(OUT_TILES // 4):
+            nc.sync.dma_start(out=w_rows[b][:], in_=w_in[b])
 
-        def widen(eng, a, t):
-            src = r8[a][:, t, :].bitcast(E4M3)
-            if eng == "v":
-                nc.vector.tensor_scalar(out=rw[a][:, t, :], in0=src, scalar1=rscale[:, a, t : t + 1], scalar2=None, op0=MULT)
+        def widen(engine, a, t):
+            src = resid_b[a][:, t, :].bitcast(E4M3)
+            scale = edit_scale[:, a, t : t + 1]
+            if engine == "vector":
+                nc.vector.tensor_scalar(out=resid_w[a][:, t, :], in0=src, scalar1=scale, scalar2=None, op0=MULT)
             else:
-                nc.scalar.activation(out=rw[a][:, t, :], in_=src, func=COPY, scale=rscale[:, a, t : t + 1])
+                nc.scalar.activation(out=resid_w[a][:, t, :], in_=src, func=COPY, scale=scale)
 
-        def copy(eng, dst, src):
-            if eng == "v":
+        def mix_resid(a, half):
+            nc.vector.tensor_copy(
+                out=resid_mix[a][:, 1024 * half : 1024 * (half + 1)].rearrange("p (c i t) -> p c t i", i=4, t=PACK),
+                in_=resid_w[a][:, :, 256 * half : 256 * (half + 1)].rearrange("p t (c i) -> p c t i", i=4),
+            )
+
+        def mix_keys(engine, g, a, m0, m1):
+            dst = keys_mix[g][a][:].rearrange("p (t m j) -> p m j t", t=PACK, j=PACK)[:, m0:m1]
+            src = keys_raw[g][a][:].rearrange("p j (m t) -> p m j t", t=PACK)[:, m0:m1]
+            if engine == "vector":
                 nc.vector.tensor_copy(out=dst, in_=src)
             else:
                 nc.scalar.copy(out=dst, in_=src)
 
-        def r_direct(eng, a, h):
-            copy(
-                eng,
-                rg[a][:, 1024 * h : 1024 * (h + 1)].rearrange("p (c i t) -> p c t i", i=4, t=4),
-                rw[a][:, :, 256 * h : 256 * (h + 1)].rearrange("p t (c i) -> p c t i", i=4),
-            )
+        def scalar_mixes_keys(g, a):
+            mix_keys("scalar", g, a, 0, SCALAR_KEYS.get((g, a), P))
 
-        def k_direct(eng, g, a, m0, m1):
-            copy(
-                eng,
-                grp[g][a][:].rearrange("p (t m j) -> p m j t", t=4, j=4)[:, m0:m1],
-                raw[g][a][:].rearrange("p j (m t) -> p m j t", t=4)[:, m0:m1],
-            )
+        def vector_mixes_keys(g, a):
+            mix_keys("vector", g, a, SCALAR_KEYS[g, a], P)
 
-        def quant(codes, scales, src, c=slice(0, 512)):
+        def quantise(codes, scales, mixed, c0, c1):
             nc.vector.quantize_mx(
-                out=codes[:, c].bitcast(E4M3X4), scales=scales[:, c], in_=src[:, 4 * c.start : 4 * c.stop]
+                out=codes[:, c0:c1].bitcast(E4M3X4), scales=scales[:, c0:c1], in_=mixed[:, PACK * c0 : PACK * c1]
             )
 
-        def quant_k(g, a):
-            quant(kc[g][a], ks[g][a], grp[g][a])
+        def quantise_resid(a, half):
+            quantise(resid_codes[a], resid_scales[a], resid_mix[a], 256 * half, 256 * (half + 1))
 
-        def quant_r(a, h):
-            quant(rc[a], rs[a], rg[a], slice(256 * h, 256 * (h + 1)))
+        def quantise_keys(g, a):
+            quantise(keys_codes[g][a], keys_scales[g][a], keys_mix[g][a], 0, PASS)
 
-        def quant_h(g):
-            quant(hc[g], hs[g], hg[g])
+        def quantise_h(g):
+            quantise(h_codes[g], h_scales[g], h_mix[g], 0, V)
 
-        def stage1(g, q, b):
-            st = bank(b, [P, 4, P], F32, "st%d%d" % (g, q))
-            v = slice(P * q, P * (q + 1))
-            for t in range(4):
-                c = slice(P * t, P * (t + 1))
-                for a in range(NA):
+        product1 = {}
+
+        def multiply1(g, quarter):
+            sums = bank_tile(PRODUCT1_BANKS[g][quarter], [P, PACK, P], F32, "sums%d%d" % (g, quarter))
+            v = slice(P * quarter, P * (quarter + 1))
+            for t in range(PACK):
+                i = slice(P * t, P * (t + 1))
+                for a in range(EDIT_PASSES):
                     nc.tensor.matmul_mx(
-                        out=st[:, t, :],
-                        lhsT=kc[g][a][:, c].bitcast(E4M3X4),
-                        lhsT_scale=ks[g][a][:, c],
-                        rhs=rc[a][:, v].bitcast(E4M3X4),
-                        rhs_scale=rs[a][:, v],
+                        out=sums[:, t, :],
+                        lhsT=keys_codes[g][a][:, i].bitcast(E4M3X4),
+                        lhsT_scale=keys_scales[g][a][:, i],
+                        rhs=resid_codes[a][:, v].bitcast(E4M3X4),
+                        rhs_scale=resid_scales[a][:, v],
                         start=(a == 0),
-                        stop=(a == NA - 1),
+                        stop=(a == EDIT_PASSES - 1),
                     )
-            return st
+            product1[g, quarter] = sums
 
-        def h_out(g, q, st):
+        def take_h(g, quarter):
             nc.vector.tensor_tensor(
-                out=hg[g][:, 512 * q : 512 * (q + 1)].rearrange("p (v t) -> p v t", t=4),
-                in0=st[:].rearrange("p t v -> p v t"),
-                in1=d1[:, g, :].unsqueeze(1).to_broadcast([P, P, 4]),
+                out=h_mix[g][:, 512 * quarter : 512 * (quarter + 1)].rearrange("p (v t) -> p v t", t=PACK),
+                in0=product1[g, quarter][:].rearrange("p t v -> p v t"),
+                in1=inv_in[:, g, :].unsqueeze(1).to_broadcast([P, P, PACK]),
                 op=MULT,
             )
 
-        acc = {}
-
-        def stage2(j, g):
+        def multiply2(sums, j, g, c0=0, c1=V):
             nc.tensor.matmul_mx(
-                out=acc[j][:],
-                lhsT=cw[g][:, 256 * j : 256 * (j + 1)].bitcast(E2M1X4),
-                lhsT_scale=cs[:, 2048 * g + P * j : 2048 * g + P * (j + 1)],
-                rhs=hc[g][:].bitcast(E4M3X4),
-                rhs_scale=hs[g][:],
+                out=sums[:],
+                lhsT=c_words[g][:, 2 * P * j : 2 * P * (j + 1)].bitcast(E2M1X4),
+                lhsT_scale=c_scales[:, D * g + P * j : D * g + P * (j + 1)],
+                rhs=h_codes[g][:, c0:c1].bitcast(E4M3X4),
+                rhs_scale=h_scales[g][:, c0:c1],
                 start=(g == 0),
-                stop=(g == NG - 1),
+                stop=(g == CHUNKS - 1),
             )
 
-        def open_acc(j, b):
-            acc[j] = bank(b, [P, V], F32, "acc%d" % j)
+        def open_tile(j):
+            return bank_tile((j + FIRST_TILE_BANK) % 8, [P, V], F32, "delta%d" % j)
 
-        def out_part(j, c0, c1, queue):
-            o = keep.tile([P, c1 - c0], F32, name="o%d_%d" % (j, c0), align_bytes=64)
+        def add_w(result, sums, j, c0, c1):
             nc.vector.scalar_tensor_tensor(
-                out=o[:],
-                in0=acc[j][:, c0:c1],
-                scalar=d2[:, j : j + 1],
-                in1=w[j // 4][:, j % 4, c0:c1],
+                out=result,
+                in0=sums,
+                scalar=inv_out[:, j : j + 1],
+                in1=w_rows[j // 4][:, j % 4, c0:c1],
                 op0=MULT,
                 op1=ADD,
             )
-            queue.dma_start(out=out[P * j : P * (j + 1), c0:c1], in_=o[:])
 
-        sts = {}
-        hx = {}
+        def store_queue(n):
+            return nc.sync if n % 2 == 0 else nc.scalar
 
-        def h_out_s(g, q):
-            hx[g, q] = keep.tile([P, 4, P], BF16, name="hx%d%d" % (g, q), align_bytes=64)
-            for t in range(4):
-                nc.scalar.activation(
-                    out=hx[g, q][:, t, :], in_=sts[g, q][:, t, :], func=COPY, scale=d1[:, g, t : t + 1]
-                )
+        def finish_tile(j, sums):
+            result = sbuf_tile([P, V], F32, "result%d" % j)
+            add_w(result[:], sums[:], j, 0, V)
+            store_queue(j).dma_start(out=out[P * j : P * (j + 1), :], in_=result[:])
 
-        def h_mix(g, q):
-            nc.vector.tensor_copy(
-                out=hg[g][:, 512 * q : 512 * (q + 1)].rearrange("p (c i t) -> p c t i", i=4, t=4),
-                in_=hx[g, q][:].rearrange("p t (c i) -> p c t i", i=4),
+        turned = bank_tile(7, [P, PACK + 1, P], BF16, "turned")
+        nc.tensor.transpose(turned[:, PACK, :], inv_rows[:, 0:P], ident[:])
+        for t in range(PACK):
+            nc.tensor.transpose(turned[:, t, :], inv_rows[:, P + t :: PACK], ident[:])
+
+        for a in range(EDIT_PASSES):
+            for t in range(PACK - 1):
+                widen("vector", a, t)
+            widen("scalar", a, PACK - 1)
+        for g in range(CHUNKS):
+            for a in range(EDIT_PASSES):
+                scalar_mixes_keys(g, a)
+
+        for a in range(EDIT_PASSES):
+            mix_resid(a, 0)
+        for a in range(EDIT_PASSES):
+            quantise_resid(a, 0)
+        vector_mixes_keys(0, 1)
+        quantise_keys(0, 0)
+        nc.vector.tensor_copy(out=inv_in[:], in_=turned[:, 0:PACK, 0:CHUNKS].rearrange("p t g -> p g t"))
+        nc.vector.tensor_copy(out=inv_out[:], in_=turned[:, PACK, 0:OUT_TILES])
+        mix_resid(0, 1)
+        quantise_keys(0, 1)
+        multiply1(0, 0)
+        multiply1(0, 1)
+        vector_mixes_keys(1, 1)
+        mix_resid(1, 1)
+        for a in range(EDIT_PASSES):
+            quantise_resid(a, 1)
+        multiply1(0, 2)
+        multiply1(0, 3)
+        for a in range(EDIT_PASSES):
+            quantise_keys(1, a)
+
+        multiply1(1, 0)
+        multiply1(1, 1)
+        take_h(0, 0)
+        multiply1(1, 2)
+        take_h(0, 1)
+        multiply1(1, 3)
+        take_h(0, 2)
+        take_h(0, 3)
+        take_h(1, 0)
+        quantise_h(0)
+        take_h(1, 1)
+
+        delta = {}
+        for j in range(EARLY_TILES):
+            delta[j] = open_tile(j)
+            multiply2(delta[j], j, 0)
+        take_h(1, 2)
+
+        for g in (2, 3):
+            if (g, 1) in SCALAR_KEYS:
+                vector_mixes_keys(g, 1)
+            for a in range(EDIT_PASSES):
+                quantise_keys(g, a)
+            multiply1(g, 0)
+            take_h(g - 1, 3)
+            quantise_h(g - 1)
+            multiply1(g, 1)
+            multiply1(g, 2)
+            take_h(g, 0)
+            multiply1(g, 3)
+            take_h(g, 1)
+            take_h(g, 2)
+            for j in range(EARLY_TILES):
+                multiply2(delta[j], j, g - 1)
+        take_h(3, 3)
+
+        delta[EARLY_TILES] = open_tile(EARLY_TILES)
+        for g in range(CHUNKS - 1):
+            multiply2(delta[EARLY_TILES], EARLY_TILES, g)
+        quantise_h(3)
+
+        for j in range(EARLY_TILES + 1):
+            multiply2(delta[j], j, CHUNKS - 1)
+            finish_tile(j, delta[j])
+        for j in range(EARLY_TILES + 1, OUT_TILES - 1):
+            delta[j] = open_tile(j)
+            for g in range(CHUNKS):
+                multiply2(delta[j], j, g)
+            finish_tile(j, delta[j])
+
+        last = OUT_TILES - 1
+        for pair in range(QUARTERS // 2):
+            result = sbuf_tile([P, 2 * P], F32, "last%d" % pair)
+            for half in range(2):
+                quarter = 2 * pair + half
+                cols = slice(P * quarter, P * (quarter + 1))
+                sums = bank_tile((last + FIRST_TILE_BANK + quarter) % 8, [P, P], F32, "delta_last%d" % quarter)
+                for g in range(CHUNKS):
+                    multiply2(sums, last, g, cols.start, cols.stop)
+                add_w(result[:, P * half : P * (half + 1)], sums[:], last, cols.start, cols.stop)
+            store_queue(pair).dma_start(
+                out=out[P * last : P * (last + 1), 2 * P * pair : 2 * P * (pair + 1)], in_=result[:]
             )
-
-        stage1_bank = [[0, 1, 2, 3], [6, 7, 0, 1], [0, 1, 0, 1], [0, 1, 0, 1]]
-
-        def s1(g, q):
-            sts[g, q] = stage1(g, q, stage1_bank[g][q])
-
-        def ev(g, q):
-            h_out(g, q, sts[g, q])
-
-        def passes(tiles, g):
-            for j in tiles:
-                stage2(j, g)
-
-        pd = bank(7, [P, 5, P], BF16, "pd")
-        nc.tensor.transpose(pd[:, 4, :], drow[:], ident[:])
-        for t in range(4):
-            nc.tensor.transpose(pd[:, t, :], drow4[:, t::4], ident[:])
-        for a in range(NA):
-            for t in range(3):
-                widen("v", a, t)
-            widen("s", a, 3)
-        k_direct("s", 0, 0, 0, 64)
-        k_direct("s", 0, 0, 64, 128)
-        k_direct("s", 0, 1, 0, 64)
-        r_direct("v", 0, 0)
-        r_direct("v", 1, 0)
-        nc.vector.tensor_copy(out=d1[:], in_=pd[:, 0:4, 0:NG].rearrange("p t g -> p g t"))
-        nc.vector.tensor_copy(out=d2[:], in_=pd[:, 4, 0:NJ])
-        quant_r(0, 0)
-        quant_r(1, 0)
-        k_direct("v", 0, 1, 64, 128)
-        quant_k(0, 0)
-        quant_k(0, 1)
-        k_direct("s", 1, 0, 0, 64)
-        k_direct("s", 1, 0, 64, 128)
-        k_direct("s", 1, 1, 0, 64)
-        s1(0, 0)
-        s1(0, 1)
-        k_direct("v", 1, 1, 64, 128)
-        r_direct("v", 0, 1)
-        r_direct("v", 1, 1)
-        quant_r(0, 1)
-        quant_r(1, 1)
-        s1(0, 2)
-        s1(0, 3)
-        quant_k(1, 0)
-        quant_k(1, 1)
-        s1(1, 0)
-        s1(1, 1)
-        for a in range(NA):
-            k_direct("s", 2, a, 0, 64)
-            k_direct("s", 2, a, 64, 128)
-        ev(0, 0)
-        s1(1, 2)
-        ev(0, 1)
-        s1(1, 3)
-        ev(0, 2)
-        ev(0, 3)
-        ev(1, 0)
-        quant_h(0)
-        ev(1, 1)
-        for j in range(6):
-            open_acc(j, 2 + j)
-        passes(range(6), 0)
-        ev(1, 2)
-        quant_k(2, 0)
-        quant_k(2, 1)
-        for a in range(NA):
-            k_direct("s", 3, a, 0, 64)
-            k_direct("s", 3, a, 64, 128)
-        s1(2, 0)
-        ev(1, 3)
-        quant_h(1)
-        s1(2, 1)
-        s1(2, 2)
-        ev(2, 0)
-        s1(2, 3)
-        ev(2, 1)
-        ev(2, 2)
-        passes(range(6), 1)
-        quant_k(3, 0)
-        quant_k(3, 1)
-        s1(3, 0)
-        ev(2, 3)
-        quant_h(2)
-        s1(3, 1)
-        s1(3, 2)
-        ev(3, 0)
-        s1(3, 3)
-        h_out_s(3, 1)
-        ev(3, 2)
-        h_out_s(3, 3)
-        h_mix(3, 1)
-        h_mix(3, 3)
-        passes(range(6), 2)
-        bank_of = [2, 3, 4, 5, 6, 7, 0, 1]
-        open_acc(6, 0)
-        for g in range(3):
-            stage2(6, g)
-        quant_h(3)
-        for j in range(7):
-            stage2(j, 3)
-            out_part(j, 0, V, nc.sync if j % 2 == 0 else nc.scalar)
-        for j in range(7, NJ):
-            open_acc(j, bank_of[j % 8])
-            for g in range(NG):
-                stage2(j, g)
-            if j < NJ - 1:
-                out_part(j, 0, V, nc.sync if j % 2 == 0 else nc.scalar)
-            else:
-                out_part(j, 0, V // 2, nc.sync)
-                out_part(j, V // 2, V, nc.scalar)

from contextlib import ExitStack

import concourse.mybir as mybir
from concourse.masks import make_identity

F32 = mybir.dt.float32
BF16 = mybir.dt.bfloat16
U32 = mybir.dt.uint32
U8 = mybir.dt.uint8
I32 = mybir.dt.int32
E4M3 = mybir.dt.float8_e4m3fn
E4M3X4 = mybir.dt.float8_e4m3fn_x4
E2M1X4 = mybir.dt.float4_e2m1fn_x4
MULT = mybir.AluOpType.mult
ADD = mybir.AluOpType.add
COPY = mybir.ActivationFunctionType.Copy

E, D, V = 1024, 2048, 512
P = 128
PACK = 4
PASS = P * PACK
EDIT_PASSES = E // PASS
CHUNKS = D // PASS
OUT_TILES = D // P
QUARTERS = V // P

FLOPS = 2 * E * D * V + 2 * D * D * V

SCALAR_KEYS = {(0, 1): 64, (1, 1): 64, (2, 1): 96}

PRODUCT1_BANKS = [[0, 1, 2, 3], [6, 7, 0, 1], [0, 1, 0, 1], [0, 1, 0, 1]]
EARLY_TILES = 6
FIRST_TILE_BANK = 2


def tile_memit_weight_edit_s13_kernel(
    tc, keys, resid_bytes, resid_scale, inv_std, cinv_words, cinv_scales, w_old, out
):
    nc = tc.nc
    with ExitStack() as ctx:
        keep = ctx.enter_context(tc.tile_pool(name="keep", bufs=1))
        psum = ctx.enter_context(tc.psum_pool(name="psum", bufs=1))

        def sbuf_tile(shape, dtype, name):
            return keep.tile(shape, dtype, name=name, align_bytes=64)

        def bank_tile(bank, shape, dtype, name):
            return psum.tile(shape, dtype, name=name, tag="bank%d" % bank)

        def per_keys(shape, dtype, name):
            return [
                [sbuf_tile(shape, dtype, "%s%d%d" % (name, g, a)) for a in range(EDIT_PASSES)] for g in range(CHUNKS)
            ]

        keys_raw = per_keys([P, PACK, PASS], BF16, "keys_raw")
        keys_mix = per_keys([P, PACK * PASS], BF16, "keys_mix")
        keys_codes = per_keys([P, PASS], U32, "keys_codes")
        keys_scales = per_keys([P, PASS], U8, "keys_scales")
        resid_b = [sbuf_tile([P, PACK, V], U8, "resid_b%d" % a) for a in range(EDIT_PASSES)]
        resid_w = [sbuf_tile([P, PACK, V], BF16, "resid_w%d" % a) for a in range(EDIT_PASSES)]
        resid_mix = [sbuf_tile([P, PACK * V], BF16, "resid_mix%d" % a) for a in range(EDIT_PASSES)]
        resid_codes = [sbuf_tile([P, V], U32, "resid_codes%d" % a) for a in range(EDIT_PASSES)]
        resid_scales = [sbuf_tile([P, V], U8, "resid_scales%d" % a) for a in range(EDIT_PASSES)]
        h_mix = [sbuf_tile([P, PACK * V], BF16, "h_mix%d" % g) for g in range(CHUNKS)]
        h_codes = [sbuf_tile([P, V], U32, "h_codes%d" % g) for g in range(CHUNKS)]
        h_scales = [sbuf_tile([P, V], U8, "h_scales%d" % g) for g in range(CHUNKS)]
        c_words = [sbuf_tile([P, 2 * D], U8, "c_words%d" % g) for g in range(CHUNKS)]
        c_scales = sbuf_tile([P, CHUNKS * D], U8, "c_scales")
        w_rows = [sbuf_tile([P, 4, V], BF16, "w_rows%d" % b) for b in range(OUT_TILES // 4)]
        ident = sbuf_tile([P, P], BF16, "ident")
        edit_scale = sbuf_tile([P, EDIT_PASSES, PACK], F32, "edit_scale")
        inv_rows = sbuf_tile([P, P + PASS], BF16, "inv_rows")
        inv_in = sbuf_tile([P, CHUNKS, PACK], F32, "inv_in")
        inv_out = sbuf_tile([P, OUT_TILES], F32, "inv_out")
        zero = sbuf_tile([P, 1], F32, "zero")
        warm = sbuf_tile([P, 1], F32, "warm")

        ctx.enter_context(tc.manual_schedule())

        nc.gpsimd.memset(inv_rows[:], 0.0)
        nc.gpsimd.memset(zero[:], 0.0)
        make_identity(nc, ident[:])
        nc.gpsimd.memset(c_scales[:].bitcast(I32), 0)
        nc.scalar.dma_start(out=edit_scale[:], in_=resid_scale.rearrange("(a p t) o -> p a (t o)", a=EDIT_PASSES, t=PACK))
        nc.scalar.dma_start(out=inv_rows[0:OUT_TILES, 0:P], in_=inv_std.rearrange("(j p) -> j p", p=P))
        nc.scalar.dma_start(out=inv_rows[0:CHUNKS, P:], in_=inv_std.rearrange("(g c) -> g c", g=CHUNKS))
        nc.scalar.activation(out=warm[:], in_=zero[:], func=COPY)

        keys_in = keys.rearrange("(a p t) i -> a p t i", a=EDIT_PASSES, t=PACK)
        resid_in = resid_bytes.rearrange("(a p t) v -> a p t v", a=EDIT_PASSES, t=PACK)
        w_in = w_old.rearrange("(b q p) v -> b p q v", q=4, p=P)
        c_scales_in = cinv_scales.bitcast(I32)
        c_scales_words = c_scales[:].bitcast(I32)

        def load_keys(g):
            for a in range(EDIT_PASSES):
                nc.sync.dma_start(out=keys_raw[g][a][:], in_=keys_in[a][:, :, PASS * g : PASS * (g + 1)])

        def load_c_scales(g):
            for q in range(4):
                nc.sync.dma_start(
                    out=c_scales_words[32 * q : 32 * q + 4, 512 * g : 512 * (g + 2)].rearrange("p (g n) -> p g n", g=2),
                    in_=c_scales_in[g : g + 2, 4 * q : 4 * q + 4, :].rearrange("g q n -> q g n"),
                )

        def load_c_words(g):
            nc.sync.dma_start(out=c_words[g][:], in_=cinv_words[g])

        for a in range(EDIT_PASSES):
            nc.sync.dma_start(out=resid_b[a][:], in_=resid_in[a])
        load_keys(0)
        load_keys(1)
        load_keys(2)
        load_c_scales(0)
        load_c_words(0)
        load_keys(3)
        load_c_words(1)
        load_c_scales(2)
        load_c_words(2)
        load_c_words(3)
        for b in range(OUT_TILES // 4):
            nc.sync.dma_start(out=w_rows[b][:], in_=w_in[b])

        def widen(engine, a, t):
            src = resid_b[a][:, t, :].bitcast(E4M3)
            scale = edit_scale[:, a, t : t + 1]
            if engine == "vector":
                nc.vector.tensor_scalar(out=resid_w[a][:, t, :], in0=src, scalar1=scale, scalar2=None, op0=MULT)
            else:
                nc.scalar.activation(out=resid_w[a][:, t, :], in_=src, func=COPY, scale=scale)

        def mix_resid(a, half):
            nc.vector.tensor_copy(
                out=resid_mix[a][:, 1024 * half : 1024 * (half + 1)].rearrange("p (c i t) -> p c t i", i=4, t=PACK),
                in_=resid_w[a][:, :, 256 * half : 256 * (half + 1)].rearrange("p t (c i) -> p c t i", i=4),
            )

        def mix_keys(engine, g, a, m0, m1):
            dst = keys_mix[g][a][:].rearrange("p (t m j) -> p m j t", t=PACK, j=PACK)[:, m0:m1]
            src = keys_raw[g][a][:].rearrange("p j (m t) -> p m j t", t=PACK)[:, m0:m1]
            if engine == "vector":
                nc.vector.tensor_copy(out=dst, in_=src)
            else:
                nc.scalar.copy(out=dst, in_=src)

        def scalar_mixes_keys(g, a):
            mix_keys("scalar", g, a, 0, SCALAR_KEYS.get((g, a), P))

        def vector_mixes_keys(g, a):
            mix_keys("vector", g, a, SCALAR_KEYS[g, a], P)

        def quantise(codes, scales, mixed, c0, c1):
            nc.vector.quantize_mx(
                out=codes[:, c0:c1].bitcast(E4M3X4), scales=scales[:, c0:c1], in_=mixed[:, PACK * c0 : PACK * c1]
            )

        def quantise_resid(a, half):
            quantise(resid_codes[a], resid_scales[a], resid_mix[a], 256 * half, 256 * (half + 1))

        def quantise_keys(g, a):
            quantise(keys_codes[g][a], keys_scales[g][a], keys_mix[g][a], 0, PASS)

        def quantise_h(g):
            quantise(h_codes[g], h_scales[g], h_mix[g], 0, V)

        product1 = {}

        def multiply1(g, quarter):
            sums = bank_tile(PRODUCT1_BANKS[g][quarter], [P, PACK, P], F32, "sums%d%d" % (g, quarter))
            v = slice(P * quarter, P * (quarter + 1))
            for t in range(PACK):
                i = slice(P * t, P * (t + 1))
                for a in range(EDIT_PASSES):
                    nc.tensor.matmul_mx(
                        out=sums[:, t, :],
                        lhsT=keys_codes[g][a][:, i].bitcast(E4M3X4),
                        lhsT_scale=keys_scales[g][a][:, i],
                        rhs=resid_codes[a][:, v].bitcast(E4M3X4),
                        rhs_scale=resid_scales[a][:, v],
                        start=(a == 0),
                        stop=(a == EDIT_PASSES - 1),
                    )
            product1[g, quarter] = sums

        def take_h(g, quarter):
            nc.vector.tensor_tensor(
                out=h_mix[g][:, 512 * quarter : 512 * (quarter + 1)].rearrange("p (v t) -> p v t", t=PACK),
                in0=product1[g, quarter][:].rearrange("p t v -> p v t"),
                in1=inv_in[:, g, :].unsqueeze(1).to_broadcast([P, P, PACK]),
                op=MULT,
            )

        def multiply2(sums, j, g, c0=0, c1=V):
            nc.tensor.matmul_mx(
                out=sums[:],
                lhsT=c_words[g][:, 2 * P * j : 2 * P * (j + 1)].bitcast(E2M1X4),
                lhsT_scale=c_scales[:, D * g + P * j : D * g + P * (j + 1)],
                rhs=h_codes[g][:, c0:c1].bitcast(E4M3X4),
                rhs_scale=h_scales[g][:, c0:c1],
                start=(g == 0),
                stop=(g == CHUNKS - 1),
            )

        def open_tile(j):
            return bank_tile((j + FIRST_TILE_BANK) % 8, [P, V], F32, "delta%d" % j)

        def add_w(result, sums, j, c0, c1):
            nc.vector.scalar_tensor_tensor(
                out=result,
                in0=sums,
                scalar=inv_out[:, j : j + 1],
                in1=w_rows[j // 4][:, j % 4, c0:c1],
                op0=MULT,
                op1=ADD,
            )

        def store_queue(n):
            return nc.sync if n % 2 == 0 else nc.scalar

        def finish_tile(j, sums):
            result = sbuf_tile([P, V], F32, "result%d" % j)
            add_w(result[:], sums[:], j, 0, V)
            store_queue(j).dma_start(out=out[P * j : P * (j + 1), :], in_=result[:])

        turned = bank_tile(7, [P, PACK + 1, P], BF16, "turned")
        nc.tensor.transpose(turned[:, PACK, :], inv_rows[:, 0:P], ident[:])
        for t in range(PACK):
            nc.tensor.transpose(turned[:, t, :], inv_rows[:, P + t :: PACK], ident[:])

        for a in range(EDIT_PASSES):
            for t in range(PACK - 1):
                widen("vector", a, t)
            widen("scalar", a, PACK - 1)
        for g in range(CHUNKS):
            for a in range(EDIT_PASSES):
                scalar_mixes_keys(g, a)

        for a in range(EDIT_PASSES):
            mix_resid(a, 0)
        for a in range(EDIT_PASSES):
            quantise_resid(a, 0)
        vector_mixes_keys(0, 1)
        quantise_keys(0, 0)
        nc.vector.tensor_copy(out=inv_in[:], in_=turned[:, 0:PACK, 0:CHUNKS].rearrange("p t g -> p g t"))
        nc.vector.tensor_copy(out=inv_out[:], in_=turned[:, PACK, 0:OUT_TILES])
        mix_resid(0, 1)
        quantise_keys(0, 1)
        multiply1(0, 0)
        multiply1(0, 1)
        vector_mixes_keys(1, 1)
        mix_resid(1, 1)
        for a in range(EDIT_PASSES):
            quantise_resid(a, 1)
        multiply1(0, 2)
        multiply1(0, 3)
        for a in range(EDIT_PASSES):
            quantise_keys(1, a)

        multiply1(1, 0)
        multiply1(1, 1)
        take_h(0, 0)
        multiply1(1, 2)
        take_h(0, 1)
        multiply1(1, 3)
        take_h(0, 2)
        take_h(0, 3)
        take_h(1, 0)
        quantise_h(0)
        take_h(1, 1)

        delta = {}
        for j in range(EARLY_TILES):
            delta[j] = open_tile(j)
            multiply2(delta[j], j, 0)
        take_h(1, 2)

        for g in (2, 3):
            if (g, 1) in SCALAR_KEYS:
                vector_mixes_keys(g, 1)
            for a in range(EDIT_PASSES):
                quantise_keys(g, a)
            multiply1(g, 0)
            take_h(g - 1, 3)
            quantise_h(g - 1)
            multiply1(g, 1)
            multiply1(g, 2)
            take_h(g, 0)
            multiply1(g, 3)
            take_h(g, 1)
            take_h(g, 2)
            for j in range(EARLY_TILES):
                multiply2(delta[j], j, g - 1)
        take_h(3, 3)

        delta[EARLY_TILES] = open_tile(EARLY_TILES)
        for g in range(CHUNKS - 1):
            multiply2(delta[EARLY_TILES], EARLY_TILES, g)
        quantise_h(3)

        for j in range(EARLY_TILES + 1):
            multiply2(delta[j], j, CHUNKS - 1)
            finish_tile(j, delta[j])
        for j in range(EARLY_TILES + 1, OUT_TILES - 1):
            delta[j] = open_tile(j)
            for g in range(CHUNKS):
                multiply2(delta[j], j, g)
            finish_tile(j, delta[j])

        last = OUT_TILES - 1
        for pair in range(QUARTERS // 2):
            result = sbuf_tile([P, 2 * P], F32, "last%d" % pair)
            for half in range(2):
                quarter = 2 * pair + half
                cols = slice(P * quarter, P * (quarter + 1))
                sums = bank_tile((last + FIRST_TILE_BANK + quarter) % 8, [P, P], F32, "delta_last%d" % quarter)
                for g in range(CHUNKS):
                    multiply2(sums, last, g, cols.start, cols.stop)
                add_w(result[:, P * half : P * (half + 1)], sums[:], last, cols.start, cols.stop)
            store_queue(pair).dma_start(
                out=out[P * last : P * (last + 1), 2 * P * pair : 2 * P * (pair + 1)], in_=result[:]
            )
